import numpy as np
import ml_dtypes


def mxq(x, axis, fmt="e4m3"):
    dtype, down = {"e4m3": (ml_dtypes.float8_e4m3fn, 7), "e5m2": (ml_dtypes.float8_e5m2, 14)}[fmt]
    v = np.moveaxis(np.asarray(x, np.float32).astype(ml_dtypes.bfloat16).astype(np.float64), axis, -1)
    blocks = v.reshape(v.shape[:-1] + (-1, 32))
    amax = np.abs(blocks).max(-1, keepdims=True)
    byte = np.maximum(np.where(amax > 0, np.frexp(amax)[1] - 1 + 127, 0) - down, 1)
    scale = np.exp2(byte - 127.0)
    codes = (blocks / scale).astype(np.float32).astype(dtype).astype(np.float64)
    return np.moveaxis((codes * scale).reshape(v.shape), -1, axis)


WIDE = False


def mx_kscale(k):
    if not WIDE:
        return np.ones(k)
    levels = np.array([10, -10, 5, -5, 0])
    if k % 512:
        return np.exp2(np.random.permutation(np.resize(levels, k // 32))).repeat(32)
    a = np.empty((k // 512, 16))
    for p in range(k // 512):
        a[p, :8] = np.random.permutation(np.resize(levels, 8))
        for g in range(8):
            far = levels[np.abs(levels - a[p, g]) >= 10]
            a[p, g + 8] = far[np.random.randint(len(far))]
    return np.exp2(a.ravel()).repeat(32)


def f64(x):
    return np.asarray(x).astype(np.float64)


def striped(idx):
    return np.tile(idx.reshape(-1, 16).T, (8, 1)).astype(np.uint16)


def unstriped(offs):
    return offs[:16].T.reshape(-1).astype(np.int64)


def gelu(v):
    return 0.5 * v * (1.0 + np.tanh(np.sqrt(2.0 / np.pi) * (v + 0.044715 * v**3)))


K, T, E, C, H, N = 512, 512, 4, 256, 1024, 512


def by_expert(wq, xq):
    return np.concatenate([wq[e].T @ xq[:, e * C:(e + 1) * C] for e in range(E)], axis=1)


def setup_inputs():
    n = np.random.standard_normal
    s = mx_kscale(K)[:, None]
    u = mx_kscale(H)
    first = np.random.permutation(np.repeat(np.arange(E), T // E))
    second = (first + 1 + np.random.permutation(np.repeat(np.arange(E - 1), -(-T // (E - 1)))[:T])) % E
    while np.bincount(second, minlength=E).max() != T // E:
        load = np.bincount(second, minlength=E); hi, lo = int(load.argmax()), int(load.argmin())
        t = np.flatnonzero((second == hi) & (first != lo))[0]; second[t] = lo
    slot_token = np.empty(E * C, np.int64); pos = np.empty((2, T), np.int64); fill = np.zeros(E, np.int64)
    place = np.stack([np.random.permutation(C) for _ in range(E)])
    for r, deal in enumerate((first, second)):
        for t in np.random.permutation(T):
            e = deal[t]; j = e * C + place[e, fill[e]]; fill[e] += 1; slot_token[j] = t; pos[r, t] = j
    g = np.random.uniform(0.2, 0.8, T)
    return {
        "xT": (n((K, T)) * s).astype(np.float32),
        "w1": (n((E, K, H)) / np.sqrt(K) / s[None] * u[None, None, :]).astype(np.float32),
        "w2": (n((E, H, N)) / np.sqrt(H) / u[None, :, None]).astype(np.float32),
        "gate": np.stack([np.tile(g, (N, 1)), np.tile(1.0 - g, (N, 1))]).astype(np.float32),
        "offs": striped(slot_token),
        "pos1": striped(pos[0]),
        "pos2": striped(pos[1]),
    }


def reference(xT, w1, w2, gate, offs, pos1, pos2):
    idx = unstriped(offs)
    xq = mxq(f64(xT)[:, idx], 0, "e4m3")
    h = gelu(by_expert(mxq(f64(w1), 1, "e4m3"), xq))
    y = by_expert(mxq(f64(w2), 1, "e4m3"), mxq(h, 0, "e4m3"))
    return f64(gate[0]) * y[:, unstriped(pos1)] + f64(gate[1]) * y[:, unstriped(pos2)]

@@ -1,0 +1,227 @@
+from contextlib import ExitStack
+
+import concourse.mybir as mybir
+
+K, T, E, C, H, N = 512, 512, 4, 256, 1024, 512
+FLOPS = 2 * E * C * (K * H + H * N)
+
+F32 = mybir.dt.float32
+BF16 = mybir.dt.bfloat16
+U32 = mybir.dt.uint32
+U16 = mybir.dt.uint16
+U8 = mybir.dt.uint8
+FP8X4 = mybir.dt.float8_e4m3fn_x4
+GELU = mybir.ActivationFunctionType.Gelu_apprx_tanh
+MULT = mybir.AluOpType.mult
+ADD = mybir.AluOpType.add
+
+P = 128
+RAW_BUFS = 6
+GRP_BUFS = 3
+ENG_X = ("v", "s", "s", "s")
+ENG_W1 = (("s", "s"), ("s", "s"), ("v", "v"), ("v", "v"))
+ENG_W2 = (("v", "v"), ("v", "s"), ("s", "v"))
+ENG_LAST0 = "v"
+ENG_LAST1 = ("v", "s", "s", "v")
+ENG_Y = ("s", "s")
+WIDE_Q = True
+
+
+def tile_routed_moe_kernel(tc, xT, w1, w2, gate, offs, pos1, pos2, out):
+    nc = tc.nc
+
+    def copy_on(engine, dst, src):
+        if engine == "v":
+            nc.vector.tensor_copy(out=dst, in_=src)
+        else:
+            nc.scalar.copy(out=dst, in_=src)
+
+    with ExitStack() as ctx:
+        lists = ctx.enter_context(tc.tile_pool(name="lists", bufs=1))
+        keep = ctx.enter_context(tc.tile_pool(name="keep", bufs=1))
+        raw = ctx.enter_context(tc.tile_pool(name="raw", bufs=RAW_BUFS))
+        grp = ctx.enter_context(tc.tile_pool(name="grp", bufs=GRP_BUFS))
+        xstage = ctx.enter_context(tc.tile_pool(name="xstage", bufs=2))
+        hstage = ctx.enter_context(tc.tile_pool(name="hstage", bufs=2))
+        fin = ctx.enter_context(tc.tile_pool(name="fin", bufs=2))
+        ps1 = ctx.enter_context(tc.psum_pool(name="ps1", bufs=4))
+        ps2 = ctx.enter_context(tc.psum_pool(name="ps2", bufs=4))
+
+        warm_in = keep.tile([P, 8], F32, name="warm_in")
+        warm_out = keep.tile([P, 8], F32, name="warm_out")
+        nc.gpsimd.memset(warm_in[:], 0.0)
+        nc.scalar.activation(out=warm_out[:], in_=warm_in[:], func=GELU)
+
+        offs_t = lists.tile([P, E * C // 16], U16, name="offs_t")
+        nc.sync.dma_start(offs_t[:], offs)
+        planes = []
+        x_view = xT.rearrange("(p t) n -> p t n", t=4)
+        for t in range(4):
+            plane = keep.tile([P, T], F32, name="plane%d" % t)
+            nc.sync.dma_start(plane[:], x_view[:, t, :])
+            planes.append(plane)
+
+        raw_w1 = {}
+        raw_w2 = {}
+        gates = {}
+
+        def load_w1(e, pieces):
+            r = raw.tile([P, 4, H], F32, name="rawt")
+            src = w1[e].rearrange("(p j) c -> p j c", j=4)
+            width = H // pieces
+            for i in range(pieces):
+                nc.sync.dma_start(r[:, :, i * width:(i + 1) * width], src[:, :, i * width:(i + 1) * width])
+            raw_w1[e] = r
+
+        def load_w2(e):
+            r = raw.tile([P, 2, 4, N], F32, name="rawt")
+            for g in range(2):
+                nc.sync.dma_start(r[:, g], w2[e][g * 512:(g + 1) * 512, :].rearrange("(p j) n -> p j n", j=4))
+            raw_w2[e] = r
+
+        def load_gates():
+            r = raw.tile([P, 4, 2, T], F32, name="rawt")
+            for m in range(4):
+                nc.sync.dma_start(r[:, m], gate[:, m * P:(m + 1) * P, :].rearrange("r p t -> p r t"))
+                gates[m] = r[:, m]
+
+        load_w1(0, 2)
+        load_w1(1, 1)
+        pos1_t = lists.tile([P, T // 16], U16, name="pos1_t")
+        nc.sync.dma_start(pos1_t[:], pos1)
+        pos2_t = lists.tile([P, T // 16], U16, name="pos2_t")
+        nc.sync.dma_start(pos2_t[:], pos2)
+        load_w1(2, 1)
+        load_w1(3, 1)
+        load_w2(0)
+        load_w2(1)
+
+        xc, xs, w1c, w1s, w2c, w2s, hc, hs = {}, {}, {}, {}, {}, {}, {}, {}
+        y = [keep.tile([P, E * C], F32, name="y%d" % m) for m in range(4)]
+
+        def x_path(e):
+            g4 = xstage.tile([P, 4, C], F32, name="g4")
+            for t in range(4):
+                nc.vector.tensor_copy(g4[:, t, :], planes[t][:].indirect(offs_t[:, e * (C // 16):(e + 1) * (C // 16)]))
+            xb = xstage.tile([P, C, 4], BF16, name="xb", align_bytes=64)
+            copy_on(ENG_X[e], xb[:], g4[:].rearrange("p t n -> p n t"))
+            xc[e] = keep.tile([P, C], U32, name="xc%d" % e, align_bytes=64)
+            xs[e] = keep.tile([P, C], U8, name="xs%d" % e, align_bytes=64)
+            nc.vector.quantize_mx(out=xc[e][:].bitcast(FP8X4), scales=xs[e][:], in_=xb[:].rearrange("p n t -> p (n t)"))
+
+        def w1_path(e):
+            w1c[e] = keep.tile([P, H], U32, name="w1c%d" % e, align_bytes=64)
+            w1s[e] = keep.tile([P, H], U8, name="w1s%d" % e, align_bytes=64)
+            gb = grp.tile([P, 2, 4, P, 4], BF16, name="gb", align_bytes=64)
+            for g2 in range(2):
+                copy_on(
+                    ENG_W1[e][g2],
+                    gb[:, g2].rearrange("p t m j -> p m t j"),
+                    raw_w1[e][:, :, g2 * 512:(g2 + 1) * 512].rearrange("p j (m t) -> p m t j", t=4),
+                )
+            nc.vector.quantize_mx(out=w1c[e][:].bitcast(FP8X4), scales=w1s[e][:], in_=gb[:].rearrange("p g t m j -> p (g t m j)"))
+
+        def w2_tiles(e):
+            w2c[e] = keep.tile([P, 2 * N], U32, name="w2c%d" % e, align_bytes=64)
+            w2s[e] = keep.tile([P, 2 * N], U8, name="w2s%d" % e, align_bytes=64)
+
+        def w2_path(e):
+            w2_tiles(e)
+            gb = grp.tile([P, 2, N, 4], BF16, name="gb", align_bytes=64)
+            for g in range(2):
+                copy_on(ENG_W2[e][g], gb[:, g], raw_w2[e][:, g].rearrange("p j n -> p n j"))
+            nc.vector.quantize_mx(out=w2c[e][:].bitcast(FP8X4), scales=w2s[e][:], in_=gb[:].rearrange("p g n j -> p (g n j)"))
+
+        def layer1(e):
+            hb = hstage.tile([P, 2, C, 4], BF16, name="hb", align_bytes=64)
+            for g2 in range(2):
+                for s in range(2):
+                    acc = ps1.tile([P, 4, P], F32, name="acc1")
+                    for t in range(4):
+                        cols = slice(g2 * 512 + t * P, g2 * 512 + (t + 1) * P)
+                        nc.tensor.matmul_mx(
+                            out=acc[:, t, :],
+                            lhsT=w1c[e][:, cols].bitcast(FP8X4),
+                            lhsT_scale=w1s[e][:, cols],
+                            rhs=xc[e][:, s * P:(s + 1) * P].bitcast(FP8X4),
+                            rhs_scale=xs[e][:, s * P:(s + 1) * P],
+                            start=True,
+                            stop=True,
+                        )
+                    nc.scalar.activation(out=hb[:, g2, s * P:(s + 1) * P, :], in_=acc[:].rearrange("p t n -> p n t"), func=GELU)
+            hc[e] = keep.tile([P, 2 * C], U32, name="hc%d" % e, align_bytes=64)
+            hs[e] = keep.tile([P, 2 * C], U8, name="hs%d" % e, align_bytes=64)
+            nc.vector.quantize_mx(out=hc[e][:].bitcast(FP8X4), scales=hs[e][:], in_=hb[:].rearrange("p g n t -> p (g n t)"))
+
+        def l2_pass(acc, e, g, m):
+            cols = slice(g * N + m * P, g * N + (m + 1) * P)
+            nc.tensor.matmul_mx(
+                out=acc,
+                lhsT=w2c[e][:, cols].bitcast(FP8X4),
+                lhsT_scale=w2s[e][:, cols],
+                rhs=hc[e][:, g * C:(g + 1) * C].bitcast(FP8X4),
+                rhs_scale=hs[e][:, g * C:(g + 1) * C],
+                start=(g == 0),
+                stop=(g == 1),
+            )
+
+        banks = {}
+
+        def layer2(e, m):
+            if e % 2 == 0:
+                banks[m] = ps2.tile([P, 2, C], F32, name="acc2")
+            for g in range(2):
+                l2_pass(banks[m][:, e % 2, :], e, g, m)
+            if e % 2 == 1:
+                evacuate(e, m)
+
+        def evacuate(e, m):
+            copy_on(ENG_Y[e // 2], y[m][:, (e - 1) * C:(e + 1) * C], banks[m][:].rearrange("p a c -> p (a c)"))
+
+        def combine(m):
+            a = fin.tile([P, T], F32, name="prod_a")
+            b = fin.tile([P, T], F32, name="prod_b")
+            o = fin.tile([P, T], F32, name="res")
+            nc.vector.tensor_tensor(a[:], y[m][:].indirect(pos1_t[:]), gates[m][:, 0, :], MULT)
+            nc.vector.tensor_tensor(b[:], y[m][:].indirect(pos2_t[:]), gates[m][:, 1, :], MULT)
+            nc.vector.tensor_tensor(o[:], a[:], b[:], ADD)
+            nc.sync.dma_start(out[m * P:(m + 1) * P, :], o[:])
+
+        x_path(0)
+        w1_path(0)
+        load_w2(2)
+        x_path(1)
+        layer1(0)
+        w1_path(1)
+        load_w2(3)
+        x_path(2)
+        layer1(1)
+        w1_path(2)
+        load_gates()
+        x_path(3)
+        layer1(2)
+        w1_path(3)
+        layer1(3)
+        for e in range(E - 1):
+            w2_path(e)
+            for m in range(4):
+                layer2(e, m)
+        e = E - 1
+        w2_tiles(e)
+        gb0 = grp.tile([P, N, 4], BF16, name="gb", align_bytes=64)
+        copy_on(ENG_LAST0, gb0[:], raw_w2[e][:, 0].rearrange("p j n -> p n j"))
+        nc.vector.quantize_mx(out=w2c[e][:, 0:N].bitcast(FP8X4), scales=w2s[e][:, 0:N], in_=gb0[:].rearrange("p n j -> p (n j)"))
+        for m in range(4):
+            l2_pass(banks[m][:, 1, :], e, 0, m)
+        gb1 = grp.tile([P, N, 4], BF16, name="gb", align_bytes=64)
+        for m in range(4):
+            copy_on(ENG_LAST1[m], gb1[:, m * P:(m + 1) * P, :], raw_w2[e][:, 1, :, m * P:(m + 1) * P].rearrange("p j n -> p n j"))
+            nc.vector.quantize_mx(
+                out=w2c[e][:, N + m * P:N + (m + 1) * P].bitcast(FP8X4),
+                scales=w2s[e][:, N + m * P:N + (m + 1) * P],
+                in_=gb1[:, m * P:(m + 1) * P, :].rearrange("p n j -> p (n j)"),
+            )
+            l2_pass(banks[m][:, 1, :], e, 1, m)
+            evacuate(e, m)
+        for m in range(4):
+            combine(m)

@@ -1,6 +1,7 @@
 from contextlib import ExitStack
 
 import concourse.mybir as mybir
+from concourse.masks import make_identity
 
 K, T, E, C, H, N = 512, 512, 4, 256, 1024, 512
 FLOPS = 2 * E * C * (K * H + H * N)
@@ -17,14 +18,14 @@ ADD = mybir.AluOpType.add
 
 P = 128
 RAW_BUFS = 6
-GRP_BUFS = 3
+GRP_BUFS = 2
 ENG_X = ("v", "s", "s", "s")
 ENG_W1 = (("s", "s"), ("s", "s"), ("v", "v"), ("v", "v"))
 ENG_W2 = (("v", "v"), ("v", "s"), ("s", "v"))
 ENG_LAST0 = "v"
 ENG_LAST1 = ("v", "s", "s", "v")
 ENG_Y = ("s", "s")
-WIDE_Q = True
+PE_ADD = 3
 
 
 def tile_routed_moe_kernel(tc, xT, w1, w2, gate, offs, pos1, pos2, out):
@@ -51,6 +52,9 @@ def tile_routed_moe_kernel(tc, xT, w1, w2, gate, offs, pos1, pos2, out):
         warm_out = keep.tile([P, 8], F32, name="warm_out")
         nc.gpsimd.memset(warm_in[:], 0.0)
         nc.scalar.activation(out=warm_out[:], in_=warm_in[:], func=GELU)
+
+        ident = keep.tile([P, P], F32, name="ident")
+        make_identity(nc, ident[:])
 
         offs_t = lists.tile([P, E * C // 16], U16, name="offs_t")
         nc.sync.dma_start(offs_t[:], offs)
@@ -100,7 +104,10 @@ def tile_routed_moe_kernel(tc, xT, w1, w2, gate, offs, pos1, pos2, out):
         y = [keep.tile([P, E * C], F32, name="y%d" % m) for m in range(4)]
 
         def x_path(e):
-            g4 = xstage.tile([P, 4, C], F32, name="g4")
+            if e < 2:
+                g4 = xstage.tile([P, 4, C], F32, name="g4")
+            else:
+                g4 = grp.tile([P, 4, C], F32, name="gb", align_bytes=64)
             for t in range(4):
                 nc.vector.tensor_copy(g4[:, t, :], planes[t][:].indirect(offs_t[:, e * (C // 16):(e + 1) * (C // 16)]))
             xb = xstage.tile([P, C, 4], BF16, name="xb", align_bytes=64)
@@ -112,14 +119,15 @@ def tile_routed_moe_kernel(tc, xT, w1, w2, gate, offs, pos1, pos2, out):
         def w1_path(e):
             w1c[e] = keep.tile([P, H], U32, name="w1c%d" % e, align_bytes=64)
             w1s[e] = keep.tile([P, H], U8, name="w1s%d" % e, align_bytes=64)
-            gb = grp.tile([P, 2, 4, P, 4], BF16, name="gb", align_bytes=64)
-            for g2 in range(2):
+            gb = grp.tile([P, 4, 2 * P, 4], BF16, name="gb", align_bytes=64)
+            spans = ((0, 2 * P),) if ENG_W1[e][0] == ENG_W1[e][1] else ((0, P), (P, 2 * P))
+            for q0, q1 in spans:
                 copy_on(
-                    ENG_W1[e][g2],
-                    gb[:, g2].rearrange("p t m j -> p m t j"),
-                    raw_w1[e][:, :, g2 * 512:(g2 + 1) * 512].rearrange("p j (m t) -> p m t j", t=4),
+                    ENG_W1[e][q0 // P],
+                    gb[:, :, q0:q1, :].rearrange("p t q j -> p q t j"),
+                    raw_w1[e][:, :, 4 * q0:4 * q1].rearrange("p j (q t) -> p q t j", t=4),
                 )
-            nc.vector.quantize_mx(out=w1c[e][:].bitcast(FP8X4), scales=w1s[e][:], in_=gb[:].rearrange("p g t m j -> p (g t m j)"))
+            nc.vector.quantize_mx(out=w1c[e][:].bitcast(FP8X4), scales=w1s[e][:], in_=gb[:].rearrange("p t q j -> p (t q j)"))
 
         def w2_tiles(e):
             w2c[e] = keep.tile([P, 2 * N], U32, name="w2c%d" % e, align_bytes=64)
@@ -128,8 +136,11 @@ def tile_routed_moe_kernel(tc, xT, w1, w2, gate, offs, pos1, pos2, out):
         def w2_path(e):
             w2_tiles(e)
             gb = grp.tile([P, 2, N, 4], BF16, name="gb", align_bytes=64)
-            for g in range(2):
-                copy_on(ENG_W2[e][g], gb[:, g], raw_w2[e][:, g].rearrange("p j n -> p n j"))
+            if ENG_W2[e][0] == ENG_W2[e][1]:
+                copy_on(ENG_W2[e][0], gb[:], raw_w2[e][:].rearrange("p g j n -> p g n j"))
+            else:
+                for g in range(2):
+                    copy_on(ENG_W2[e][g], gb[:, g], raw_w2[e][:, g].rearrange("p j n -> p n j"))
             nc.vector.quantize_mx(out=w2c[e][:].bitcast(FP8X4), scales=w2s[e][:], in_=gb[:].rearrange("p g n j -> p (g n j)"))
 
         def layer1(e):
@@ -138,7 +149,7 @@ def tile_routed_moe_kernel(tc, xT, w1, w2, gate, offs, pos1, pos2, out):
                 for s in range(2):
                     acc = ps1.tile([P, 4, P], F32, name="acc1")
                     for t in range(4):
-                        cols = slice(g2 * 512 + t * P, g2 * 512 + (t + 1) * P)
+                        cols = slice(t * 256 + g2 * P, t * 256 + (g2 + 1) * P)
                         nc.tensor.matmul_mx(
                             out=acc[:, t, :],
                             lhsT=w1c[e][:, cols].bitcast(FP8X4),
@@ -184,21 +195,27 @@ def tile_routed_moe_kernel(tc, xT, w1, w2, gate, offs, pos1, pos2, out):
             o = fin.tile([P, T], F32, name="res")
             nc.vector.tensor_tensor(a[:], y[m][:].indirect(pos1_t[:]), gates[m][:, 0, :], MULT)
             nc.vector.tensor_tensor(b[:], y[m][:].indirect(pos2_t[:]), gates[m][:, 1, :], MULT)
-            nc.vector.tensor_tensor(o[:], a[:], b[:], ADD)
+            if m < PE_ADD:
+                total = ps1.tile([P, T], F32, name="acc1")
+                nc.tensor.matmul(out=total[:], lhsT=ident[:], rhs=a[:], start=True, stop=False)
+                nc.tensor.matmul(out=total[:], lhsT=ident[:], rhs=b[:], start=False, stop=True)
+                nc.scalar.copy(out=o[:], in_=total[:])
+            else:
+                nc.vector.tensor_tensor(o[:], a[:], b[:], ADD)
             nc.sync.dma_start(out[m * P:(m + 1) * P, :], o[:])
 
         x_path(0)
+        x_path(1)
         w1_path(0)
         load_w2(2)
-        x_path(1)
         layer1(0)
         w1_path(1)
         load_w2(3)
         x_path(2)
         layer1(1)
+        x_path(3)
         w1_path(2)
         load_gates()
-        x_path(3)
         layer1(2)
         w1_path(3)
         layer1(3)

@@ -111,7 +111,7 @@ def tile_routed_moe_kernel(tc, xT, w1, w2, gate, offs, pos1, pos2, out):
             for t in range(4):
                 nc.vector.tensor_copy(g4[:, t, :], planes[t][:].indirect(offs_t[:, e * (C // 16):(e + 1) * (C // 16)]))
             xb = xstage.tile([P, C, 4], BF16, name="xb", align_bytes=64)
-            copy_on(ENG_X[e], xb[:], g4[:].rearrange("p t n -> p n t"))
+            copy_on(ENG_X[e], xb[:].rearrange("p (c i) t -> p c t i", i=4), g4[:].rearrange("p t (c i) -> p c t i", i=4))
             xc[e] = keep.tile([P, C], U32, name="xc%d" % e, align_bytes=64)
             xs[e] = keep.tile([P, C], U8, name="xs%d" % e, align_bytes=64)
             nc.vector.quantize_mx(out=xc[e][:].bitcast(FP8X4), scales=xs[e][:], in_=xb[:].rearrange("p n t -> p (n t)"))
@@ -124,8 +124,8 @@ def tile_routed_moe_kernel(tc, xT, w1, w2, gate, offs, pos1, pos2, out):
             for q0, q1 in spans:
                 copy_on(
                     ENG_W1[e][q0 // P],
-                    gb[:, :, q0:q1, :].rearrange("p t q j -> p q t j"),
-                    raw_w1[e][:, :, 4 * q0:4 * q1].rearrange("p j (q t) -> p q t j", t=4),
+                    gb[:, :, q0:q1, :].rearrange("p t q j -> p q j t"),
+                    raw_w1[e][:, :, 4 * q0:4 * q1].rearrange("p j (q t) -> p q j t", t=4),
                 )
             nc.vector.quantize_mx(out=w1c[e][:].bitcast(FP8X4), scales=w1s[e][:], in_=gb[:].rearrange("p t q j -> p (t q j)"))
 
@@ -137,10 +137,10 @@ def tile_routed_moe_kernel(tc, xT, w1, w2, gate, offs, pos1, pos2, out):
             w2_tiles(e)
             gb = grp.tile([P, 2, N, 4], BF16, name="gb", align_bytes=64)
             if ENG_W2[e][0] == ENG_W2[e][1]:
-                copy_on(ENG_W2[e][0], gb[:], raw_w2[e][:].rearrange("p g j n -> p g n j"))
+                copy_on(ENG_W2[e][0], gb[:].rearrange("p g (c i) j -> p g c j i", i=4), raw_w2[e][:].rearrange("p g j (c i) -> p g c j i", i=4))
             else:
                 for g in range(2):
-                    copy_on(ENG_W2[e][g], gb[:, g], raw_w2[e][:, g].rearrange("p j n -> p n j"))
+                    copy_on(ENG_W2[e][g], gb[:, g].rearrange("p (c i) j -> p c j i", i=4), raw_w2[e][:, g].rearrange("p j (c i) -> p c j i", i=4))
             nc.vector.quantize_mx(out=w2c[e][:].bitcast(FP8X4), scales=w2s[e][:], in_=gb[:].rearrange("p g n j -> p (g n j)"))
 
         def layer1(e):
@@ -226,13 +226,13 @@ def tile_routed_moe_kernel(tc, xT, w1, w2, gate, offs, pos1, pos2, out):
         e = E - 1
         w2_tiles(e)
         gb0 = grp.tile([P, N, 4], BF16, name="gb", align_bytes=64)
-        copy_on(ENG_LAST0, gb0[:], raw_w2[e][:, 0].rearrange("p j n -> p n j"))
+        copy_on(ENG_LAST0, gb0[:].rearrange("p (c i) j -> p c j i", i=4), raw_w2[e][:, 0].rearrange("p j (c i) -> p c j i", i=4))
         nc.vector.quantize_mx(out=w2c[e][:, 0:N].bitcast(FP8X4), scales=w2s[e][:, 0:N], in_=gb0[:].rearrange("p n j -> p (n j)"))
         for m in range(4):
             l2_pass(banks[m][:, 1, :], e, 0, m)
         gb1 = grp.tile([P, N, 4], BF16, name="gb", align_bytes=64)
         for m in range(4):
-            copy_on(ENG_LAST1[m], gb1[:, m * P:(m + 1) * P, :], raw_w2[e][:, 1, :, m * P:(m + 1) * P].rearrange("p j n -> p n j"))
+            copy_on(ENG_LAST1[m], gb1[:, m * P:(m + 1) * P, :].rearrange("p (c i) j -> p c j i", i=4), raw_w2[e][:, 1, :, m * P:(m + 1) * P].rearrange("p j (c i) -> p c j i", i=4))
             nc.vector.quantize_mx(
                 out=w2c[e][:, N + m * P:N + (m + 1) * P].bitcast(FP8X4),
                 scales=w2s[e][:, N + m * P:N + (m + 1) * P],

@@ -13,15 +13,17 @@ U16 = mybir.dt.uint16
 U8 = mybir.dt.uint8
 FP8X4 = mybir.dt.float8_e4m3fn_x4
 GELU = mybir.ActivationFunctionType.Gelu_apprx_tanh
+COPY = mybir.ActivationFunctionType.Copy
 MULT = mybir.AluOpType.mult
 ADD = mybir.AluOpType.add
 
 P = 128
 RAW_BUFS = 6
-GRP_BUFS = 2
-ENG_X = ("v", "s", "s", "s")
-ENG_W1 = (("s", "s"), ("s", "s"), ("v", "v"), ("v", "v"))
-ENG_W2 = (("v", "v"), ("v", "s"), ("s", "v"))
+STEP = 512
+X_FORM = ("f", "f", "a", "a")
+W1_PIECES = (2, 1, 1, 1)
+ENG_W1 = (("v", "v"), ("v", "v"), ("v", "v"), ("v", "v"))
+ENG_W2 = (("v", "v"), ("v", "v"), ("s", "v"))
 ENG_LAST0 = "v"
 ENG_LAST1 = ("v", "s", "s", "v")
 ENG_Y = ("s", "s")
@@ -41,9 +43,10 @@ def tile_routed_moe_kernel(tc, xT, w1, w2, gate, offs, pos1, pos2, out):
         lists = ctx.enter_context(tc.tile_pool(name="lists", bufs=1))
         keep = ctx.enter_context(tc.tile_pool(name="keep", bufs=1))
         raw = ctx.enter_context(tc.tile_pool(name="raw", bufs=RAW_BUFS))
-        grp = ctx.enter_context(tc.tile_pool(name="grp", bufs=GRP_BUFS))
+        arena = ctx.enter_context(tc.tile_pool(name="arena", bufs=1))
         xstage = ctx.enter_context(tc.tile_pool(name="xstage", bufs=2))
-        hstage = ctx.enter_context(tc.tile_pool(name="hstage", bufs=2))
+        xbpool = ctx.enter_context(tc.tile_pool(name="xbpool", bufs=4))
+        hstage = ctx.enter_context(tc.tile_pool(name="hstage", bufs=3))
         fin = ctx.enter_context(tc.tile_pool(name="fin", bufs=2))
         ps1 = ctx.enter_context(tc.psum_pool(name="ps1", bufs=4))
         ps2 = ctx.enter_context(tc.psum_pool(name="ps2", bufs=4))
@@ -64,6 +67,7 @@ def tile_routed_moe_kernel(tc, xT, w1, w2, gate, offs, pos1, pos2, out):
             plane = keep.tile([P, T], F32, name="plane%d" % t)
             nc.sync.dma_start(plane[:], x_view[:, t, :])
             planes.append(plane)
+        xbf = keep.tile([P, 4, T], BF16, name="xbf")
 
         raw_w1 = {}
         raw_w2 = {}
@@ -90,7 +94,7 @@ def tile_routed_moe_kernel(tc, xT, w1, w2, gate, offs, pos1, pos2, out):
                 gates[m] = r[:, m]
 
         load_w1(0, 2)
-        load_w1(1, 1)
+        load_w1(1, 2)
         pos1_t = lists.tile([P, T // 16], U16, name="pos1_t")
         nc.sync.dma_start(pos1_t[:], pos1)
         pos2_t = lists.tile([P, T // 16], U16, name="pos2_t")
@@ -103,24 +107,37 @@ def tile_routed_moe_kernel(tc, xT, w1, w2, gate, offs, pos1, pos2, out):
         xc, xs, w1c, w1s, w2c, w2s, hc, hs = {}, {}, {}, {}, {}, {}, {}, {}
         y = [keep.tile([P, E * C], F32, name="y%d" % m) for m in range(4)]
 
-        def x_path(e):
-            if e < 2:
-                g4 = xstage.tile([P, 4, C], F32, name="g4")
-            else:
-                g4 = grp.tile([P, 4, C], F32, name="gb", align_bytes=64)
+        xbs = {}
+        g4s = {}
+        hbs = {}
+
+        def x_gather():
+            for e in range(E):
+                xbs[e] = xbpool.tile([P, C, 4], BF16, name="xb", align_bytes=64)
+                if X_FORM[e] == "a":
+                    g4s[e] = xstage.tile([P, 4, C], F32, name="g4")
             for t in range(4):
-                nc.vector.tensor_copy(g4[:, t, :], planes[t][:].indirect(offs_t[:, e * (C // 16):(e + 1) * (C // 16)]))
-            xb = xstage.tile([P, C, 4], BF16, name="xb", align_bytes=64)
-            copy_on(ENG_X[e], xb[:].rearrange("p (c i) t -> p c t i", i=4), g4[:].rearrange("p t (c i) -> p c t i", i=4))
+                nc.vector.tensor_copy(out=xbf[:, t, :], in_=planes[t][:])
+                for e in range(E):
+                    slots = offs_t[:, e * (C // 16):(e + 1) * (C // 16)]
+                    if X_FORM[e] == "a":
+                        nc.vector.tensor_copy(g4s[e][:, t, :], planes[t][:].indirect(slots))
+                    else:
+                        nc.scalar.activation(out=xbs[e][:, :, t], in_=xbf[:, t, :].indirect(slots), func=COPY)
+
+        def x_path(e):
+            xb = xbs[e]
+            if X_FORM[e] == "a":
+                copy_on("s", xb[:].rearrange("p (c i) t -> p c t i", i=4), g4s[e][:].rearrange("p t (c i) -> p c t i", i=4))
             xc[e] = keep.tile([P, C], U32, name="xc%d" % e, align_bytes=64)
-            xs[e] = keep.tile([P, C], U8, name="xs%d" % e, align_bytes=64)
+            xs[e] = arena.tile([P, C], U8, name="xs%d" % e, align_bytes=64, offset=C * e)
             nc.vector.quantize_mx(out=xc[e][:].bitcast(FP8X4), scales=xs[e][:], in_=xb[:].rearrange("p n t -> p (n t)"))
 
         def w1_path(e):
             w1c[e] = keep.tile([P, H], U32, name="w1c%d" % e, align_bytes=64)
             w1s[e] = keep.tile([P, H], U8, name="w1s%d" % e, align_bytes=64)
-            gb = grp.tile([P, 4, 2 * P, 4], BF16, name="gb", align_bytes=64)
-            spans = ((0, 2 * P),) if ENG_W1[e][0] == ENG_W1[e][1] else ((0, P), (P, 2 * P))
+            gb = arena.tile([P, 4, 2 * P, 4], BF16, name="gb%d" % e, align_bytes=64, offset=STEP * e)
+            spans = ((0, 2 * P),) if W1_PIECES[e] == 1 else ((0, P), (P, 2 * P))
             for q0, q1 in spans:
                 copy_on(
                     ENG_W1[e][q0 // P],
@@ -135,7 +152,7 @@ def tile_routed_moe_kernel(tc, xT, w1, w2, gate, offs, pos1, pos2, out):
 
         def w2_path(e):
             w2_tiles(e)
-            gb = grp.tile([P, 2, N, 4], BF16, name="gb", align_bytes=64)
+            gb = arena.tile([P, 2, N, 4], BF16, name="gb%d" % (4 + e), align_bytes=64, offset=STEP * (4 + e))
             if ENG_W2[e][0] == ENG_W2[e][1]:
                 copy_on(ENG_W2[e][0], gb[:].rearrange("p g (c i) j -> p g c j i", i=4), raw_w2[e][:].rearrange("p g j (c i) -> p g c j i", i=4))
             else:
@@ -160,9 +177,12 @@ def tile_routed_moe_kernel(tc, xT, w1, w2, gate, offs, pos1, pos2, out):
                             stop=True,
                         )
                     nc.scalar.activation(out=hb[:, g2, s * P:(s + 1) * P, :], in_=acc[:].rearrange("p t n -> p n t"), func=GELU)
+            hbs[e] = hb
+
+        def h_quant(e):
             hc[e] = keep.tile([P, 2 * C], U32, name="hc%d" % e, align_bytes=64)
-            hs[e] = keep.tile([P, 2 * C], U8, name="hs%d" % e, align_bytes=64)
-            nc.vector.quantize_mx(out=hc[e][:].bitcast(FP8X4), scales=hs[e][:], in_=hb[:].rearrange("p g n t -> p (g n t)"))
+            hs[e] = arena.tile([P, 2 * C], U8, name="hs%d" % e, align_bytes=64, offset=STEP * (2 + e))
+            nc.vector.quantize_mx(out=hc[e][:].bitcast(FP8X4), scales=hs[e][:], in_=hbs[e][:].rearrange("p g n t -> p (g n t)"))
 
         def l2_pass(acc, e, g, m):
             cols = slice(g * N + m * P, g * N + (m + 1) * P)
@@ -204,33 +224,38 @@ def tile_routed_moe_kernel(tc, xT, w1, w2, gate, offs, pos1, pos2, out):
                 nc.vector.tensor_tensor(o[:], a[:], b[:], ADD)
             nc.sync.dma_start(out[m * P:(m + 1) * P, :], o[:])
 
+        x_gather()
+        w1_path(0)
         x_path(0)
         x_path(1)
-        w1_path(0)
         load_w2(2)
         layer1(0)
         w1_path(1)
-        load_w2(3)
         x_path(2)
-        layer1(1)
         x_path(3)
+        load_w2(3)
+        layer1(1)
         w1_path(2)
+        h_quant(0)
         load_gates()
         layer1(2)
         w1_path(3)
+        h_quant(1)
         layer1(3)
         for e in range(E - 1):
             w2_path(e)
+            if e < 2:
+                h_quant(2 + e)
             for m in range(4):
                 layer2(e, m)
         e = E - 1
         w2_tiles(e)
-        gb0 = grp.tile([P, N, 4], BF16, name="gb", align_bytes=64)
+        gb0 = arena.tile([P, N, 4], BF16, name="gb7", align_bytes=64, offset=STEP * 7)
         copy_on(ENG_LAST0, gb0[:].rearrange("p (c i) j -> p c j i", i=4), raw_w2[e][:, 0].rearrange("p j (c i) -> p c j i", i=4))
         nc.vector.quantize_mx(out=w2c[e][:, 0:N].bitcast(FP8X4), scales=w2s[e][:, 0:N], in_=gb0[:].rearrange("p n j -> p (n j)"))
         for m in range(4):
             l2_pass(banks[m][:, 1, :], e, 0, m)
-        gb1 = grp.tile([P, N, 4], BF16, name="gb", align_bytes=64)
+        gb1 = arena.tile([P, N, 4], BF16, name="gb8", align_bytes=64, offset=STEP * 7 + 8 * N)
         for m in range(4):
             copy_on(ENG_LAST1[m], gb1[:, m * P:(m + 1) * P, :].rearrange("p (c i) j -> p c j i", i=4), raw_w2[e][:, 1, :, m * P:(m + 1) * P].rearrange("p j (c i) -> p c j i", i=4))
             nc.vector.quantize_mx(

@@ -23,7 +23,7 @@ STEP = 512
 X_FORM = ("f", "f", "a", "a")
 W1_PIECES = (2, 1, 1, 1)
 ENG_W1 = (("v", "v"), ("v", "v"), ("v", "v"), ("v", "v"))
-ENG_W2 = (("v", "v"), ("v", "v"), ("s", "v"))
+ENG_W2 = (("s", "v"), ("s", "v"), ("s", "v"))
 ENG_LAST0 = "v"
 ENG_LAST1 = ("v", "s", "s", "v")
 ENG_Y = ("s", "s")

@@ -24,8 +24,7 @@ X_FORM = ("f", "f", "a", "a")
 W1_PIECES = (2, 1, 1, 1)
 ENG_W1 = (("v", "v"), ("v", "v"), ("v", "v"), ("v", "v"))
 ENG_W2 = (("s", "v"), ("s", "v"), ("s", "v"))
-ENG_LAST0 = "v"
-ENG_LAST1 = ("v", "s", "s", "v")
+ENG_LAST = ("v", "s", "s", "v")
 ENG_Y = ("s", "s")
 PE_ADD = 3
 
@@ -84,7 +83,12 @@ def tile_routed_moe_kernel(tc, xT, w1, w2, gate, offs, pos1, pos2, out):
         def load_w2(e):
             r = raw.tile([P, 2, 4, N], F32, name="rawt")
             for g in range(2):
-                nc.sync.dma_start(r[:, g], w2[e][g * 512:(g + 1) * 512, :].rearrange("(p j) n -> p j n", j=4))
+                src = w2[e][g * 512:(g + 1) * 512, :].rearrange("(p j) n -> p j n", j=4)
+                if e == E - 1 and g == 1:
+                    for m in range(4):
+                        nc.sync.dma_start(r[:, g, :, m * P:(m + 1) * P], src[:, :, m * P:(m + 1) * P])
+                else:
+                    nc.sync.dma_start(r[:, g], src)
             raw_w2[e] = r
 
         def load_gates():
@@ -250,20 +254,30 @@ def tile_routed_moe_kernel(tc, xT, w1, w2, gate, offs, pos1, pos2, out):
                 layer2(e, m)
         e = E - 1
         w2_tiles(e)
-        gb0 = arena.tile([P, N, 4], BF16, name="gb7", align_bytes=64, offset=STEP * 7)
-        copy_on(ENG_LAST0, gb0[:].rearrange("p (c i) j -> p c j i", i=4), raw_w2[e][:, 0].rearrange("p j (c i) -> p c j i", i=4))
-        nc.vector.quantize_mx(out=w2c[e][:, 0:N].bitcast(FP8X4), scales=w2s[e][:, 0:N], in_=gb0[:].rearrange("p n j -> p (n j)"))
+        chunk_offset = (STEP * 7, STEP * 7 + 2048, STEP * 7 + 4096, STEP * 7)
         for m in range(4):
-            l2_pass(banks[m][:, 1, :], e, 0, m)
-        gb1 = arena.tile([P, N, 4], BF16, name="gb8", align_bytes=64, offset=STEP * 7 + 8 * N)
-        for m in range(4):
-            copy_on(ENG_LAST1[m], gb1[:, m * P:(m + 1) * P, :].rearrange("p (c i) j -> p c j i", i=4), raw_w2[e][:, 1, :, m * P:(m + 1) * P].rearrange("p j (c i) -> p c j i", i=4))
-            nc.vector.quantize_mx(
-                out=w2c[e][:, N + m * P:N + (m + 1) * P].bitcast(FP8X4),
-                scales=w2s[e][:, N + m * P:N + (m + 1) * P],
-                in_=gb1[:, m * P:(m + 1) * P, :].rearrange("p n j -> p (n j)"),
+            gc = arena.tile([P, 2, P, 4], BF16, name="gc%d" % m, align_bytes=64, offset=chunk_offset[m])
+            copy_on(
+                ENG_LAST[m],
+                gc[:].rearrange("p g (c i) j -> p g c j i", i=4),
+                raw_w2[e][:, :, :, m * P:(m + 1) * P].rearrange("p g j (c i) -> p g c j i", i=4),
             )
-            l2_pass(banks[m][:, 1, :], e, 1, m)
+            nc.vector.quantize_mx(
+                out=w2c[e][:, m * 2 * P:(m + 1) * 2 * P].bitcast(FP8X4),
+                scales=w2s[e][:, m * 2 * P:(m + 1) * 2 * P],
+                in_=gc[:].rearrange("p g n j -> p (g n j)"),
+            )
+            for g in range(2):
+                cols = slice((m * 2 + g) * P, (m * 2 + g + 1) * P)
+                nc.tensor.matmul_mx(
+                    out=banks[m][:, 1, :],
+                    lhsT=w2c[e][:, cols].bitcast(FP8X4),
+                    lhsT_scale=w2s[e][:, cols],
+                    rhs=hc[e][:, g * C:(g + 1) * C].bitcast(FP8X4),
+                    rhs_scale=hs[e][:, g * C:(g + 1) * C],
+                    start=(g == 0),
+                    stop=(g == 1),
+                )
             evacuate(e, m)
         for m in range(4):
             combine(m)

@@ -21,7 +21,7 @@ P = 128
 RAW_BUFS = 6
 STEP = 512
 X_FORM = ("f", "f", "a", "a")
-W1_PIECES = (2, 1, 1, 1)
+W1_PIECES = (1, 1, 1, 1)
 ENG_W1 = (("v", "v"), ("v", "v"), ("v", "v"), ("v", "v"))
 ENG_W2 = (("s", "v"), ("s", "v"), ("s", "v"))
 ENG_LAST = ("v", "s", "s", "v")
@@ -97,8 +97,8 @@ def tile_routed_moe_kernel(tc, xT, w1, w2, gate, offs, pos1, pos2, out):
                 nc.sync.dma_start(r[:, m], gate[:, m * P:(m + 1) * P, :].rearrange("r p t -> p r t"))
                 gates[m] = r[:, m]
 
-        load_w1(0, 2)
-        load_w1(1, 2)
+        load_w1(0, 1)
+        load_w1(1, 1)
         pos1_t = lists.tile([P, T // 16], U16, name="pos1_t")
         nc.sync.dma_start(pos1_t[:], pos1)
         pos2_t = lists.tile([P, T // 16], U16, name="pos2_t")

@@ -44,8 +44,9 @@ def tile_routed_moe_kernel(tc, xT, w1, w2, gate, offs, pos1, pos2, out):
         raw = ctx.enter_context(tc.tile_pool(name="raw", bufs=RAW_BUFS))
         arena = ctx.enter_context(tc.tile_pool(name="arena", bufs=1))
         xstage = ctx.enter_context(tc.tile_pool(name="xstage", bufs=2))
-        xbpool = ctx.enter_context(tc.tile_pool(name="xbpool", bufs=4))
-        hstage = ctx.enter_context(tc.tile_pool(name="hstage", bufs=3))
+        xbpool = ctx.enter_context(tc.tile_pool(name="xbpool", bufs=2))
+        hstage = ctx.enter_context(tc.tile_pool(name="hstage", bufs=2))
+        hfirst = ctx.enter_context(tc.tile_pool(name="hfirst", bufs=1))
         fin = ctx.enter_context(tc.tile_pool(name="fin", bufs=2))
         ps1 = ctx.enter_context(tc.psum_pool(name="ps1", bufs=4))
         ps2 = ctx.enter_context(tc.psum_pool(name="ps2", bufs=4))
@@ -60,12 +61,12 @@ def tile_routed_moe_kernel(tc, xT, w1, w2, gate, offs, pos1, pos2, out):
 
         offs_t = lists.tile([P, E * C // 16], U16, name="offs_t")
         nc.sync.dma_start(offs_t[:], offs)
-        planes = []
         x_view = xT.rearrange("(p t) n -> p t n", t=4)
-        for t in range(4):
-            plane = keep.tile([P, T], F32, name="plane%d" % t)
-            nc.sync.dma_start(plane[:], x_view[:, t, :])
-            planes.append(plane)
+        plane0 = keep.tile([P, T], F32, name="plane0")
+        nc.sync.dma_start(plane0[:], x_view[:, 0, :])
+        rest = keep.tile([P, 3, T], F32, name="planes123")
+        nc.sync.dma_start(rest[:], x_view[:, 1:4, :])
+        planes = [plane0[:]] + [rest[:, t, :] for t in range(3)]
         xbf = keep.tile([P, 4, T], BF16, name="xbf")
 
         raw_w1 = {}
@@ -85,8 +86,8 @@ def tile_routed_moe_kernel(tc, xT, w1, w2, gate, offs, pos1, pos2, out):
             for g in range(2):
                 src = w2[e][g * 512:(g + 1) * 512, :].rearrange("(p j) n -> p j n", j=4)
                 if e == E - 1 and g == 1:
-                    for m in range(4):
-                        nc.sync.dma_start(r[:, g, :, m * P:(m + 1) * P], src[:, :, m * P:(m + 1) * P])
+                    for m in range(2):
+                        nc.sync.dma_start(r[:, g, :, m * 2 * P:(m + 1) * 2 * P], src[:, :, m * 2 * P:(m + 1) * 2 * P])
                 else:
                     nc.sync.dma_start(r[:, g], src)
             raw_w2[e] = r
@@ -112,30 +113,33 @@ def tile_routed_moe_kernel(tc, xT, w1, w2, gate, offs, pos1, pos2, out):
         y = [keep.tile([P, E * C], F32, name="y%d" % m) for m in range(4)]
 
         xbs = {}
+        xpair = {}
         g4s = {}
         hbs = {}
 
         def x_gather():
+            for q in range(2):
+                xpair[q] = xbpool.tile([P, 2 * C, 4], BF16, name="xb", align_bytes=64)
             for e in range(E):
-                xbs[e] = xbpool.tile([P, C, 4], BF16, name="xb", align_bytes=64)
+                xbs[e] = xpair[e // 2][:, (e % 2) * C:(e % 2 + 1) * C, :]
                 if X_FORM[e] == "a":
                     g4s[e] = xstage.tile([P, 4, C], F32, name="g4")
             for t in range(4):
-                nc.vector.tensor_copy(out=xbf[:, t, :], in_=planes[t][:])
+                nc.vector.tensor_copy(out=xbf[:, t, :], in_=planes[t])
                 for e in range(E):
                     slots = offs_t[:, e * (C // 16):(e + 1) * (C // 16)]
                     if X_FORM[e] == "a":
-                        nc.vector.tensor_copy(g4s[e][:, t, :], planes[t][:].indirect(slots))
+                        nc.vector.tensor_copy(g4s[e][:, t, :], planes[t].indirect(slots))
                     else:
                         nc.scalar.activation(out=xbs[e][:, :, t], in_=xbf[:, t, :].indirect(slots), func=COPY)
 
-        def x_path(e):
-            xb = xbs[e]
-            if X_FORM[e] == "a":
-                copy_on("s", xb[:].rearrange("p (c i) t -> p c t i", i=4), g4s[e][:].rearrange("p t (c i) -> p c t i", i=4))
-            xc[e] = keep.tile([P, C], U32, name="xc%d" % e, align_bytes=64)
-            xs[e] = arena.tile([P, C], U8, name="xs%d" % e, align_bytes=64, offset=C * e)
-            nc.vector.quantize_mx(out=xc[e][:].bitcast(FP8X4), scales=xs[e][:], in_=xb[:].rearrange("p n t -> p (n t)"))
+        def x_path(q):
+            for e in (2 * q, 2 * q + 1):
+                if X_FORM[e] == "a":
+                    copy_on("s", xbs[e].rearrange("p (c i) t -> p c t i", i=4), g4s[e][:].rearrange("p t (c i) -> p c t i", i=4))
+            xc[q] = keep.tile([P, 2 * C], U32, name="xc%d" % q, align_bytes=64)
+            xs[q] = arena.tile([P, 2 * C], U8, name="xs%d" % q, align_bytes=64, offset=2 * C * q)
+            nc.vector.quantize_mx(out=xc[q][:].bitcast(FP8X4), scales=xs[q][:], in_=xpair[q][:].rearrange("p n t -> p (n t)"))
 
         def w1_path(e):
             w1c[e] = keep.tile([P, H], U32, name="w1c%d" % e, align_bytes=64)
@@ -156,7 +160,7 @@ def tile_routed_moe_kernel(tc, xT, w1, w2, gate, offs, pos1, pos2, out):
 
         def w2_path(e):
             w2_tiles(e)
-            gb = arena.tile([P, 2, N, 4], BF16, name="gb%d" % (4 + e), align_bytes=64, offset=STEP * (4 + e))
+            gb = arena.tile([P, 2, N, 4], BF16, name="gb%d" % (4 + e), align_bytes=64, offset=STEP * (5 + e))
             if ENG_W2[e][0] == ENG_W2[e][1]:
                 copy_on(ENG_W2[e][0], gb[:].rearrange("p g (c i) j -> p g c j i", i=4), raw_w2[e][:].rearrange("p g j (c i) -> p g c j i", i=4))
             else:
@@ -165,7 +169,12 @@ def tile_routed_moe_kernel(tc, xT, w1, w2, gate, offs, pos1, pos2, out):
             nc.vector.quantize_mx(out=w2c[e][:].bitcast(FP8X4), scales=w2s[e][:], in_=gb[:].rearrange("p g n j -> p (g n j)"))
 
         def layer1(e):
-            hb = hstage.tile([P, 2, C, 4], BF16, name="hb", align_bytes=64)
+            if e == 0:
+                hbs["pair"] = hfirst.tile([P, 2, 2, C, 4], BF16, name="hpair", align_bytes=64)
+            if e < 2:
+                hb = hbs["pair"][:, e]
+            else:
+                hb = hstage.tile([P, 2, C, 4], BF16, name="hb", align_bytes=64)
             for g2 in range(2):
                 for s in range(2):
                     acc = ps1.tile([P, 4, P], F32, name="acc1")
@@ -175,18 +184,28 @@ def tile_routed_moe_kernel(tc, xT, w1, w2, gate, offs, pos1, pos2, out):
                             out=acc[:, t, :],
                             lhsT=w1c[e][:, cols].bitcast(FP8X4),
                             lhsT_scale=w1s[e][:, cols],
-                            rhs=xc[e][:, s * P:(s + 1) * P].bitcast(FP8X4),
-                            rhs_scale=xs[e][:, s * P:(s + 1) * P],
+                            rhs=xc[e // 2][:, (e % 2) * C + s * P:(e % 2) * C + (s + 1) * P].bitcast(FP8X4),
+                            rhs_scale=xs[e // 2][:, (e % 2) * C + s * P:(e % 2) * C + (s + 1) * P],
                             start=True,
                             stop=True,
                         )
                     nc.scalar.activation(out=hb[:, g2, s * P:(s + 1) * P, :], in_=acc[:].rearrange("p t n -> p n t"), func=GELU)
             hbs[e] = hb
 
+        def h_quant_first():
+            codes = keep.tile([P, 4 * C], U32, name="hc01", align_bytes=64)
+            scales = arena.tile([P, 4 * C], U8, name="hs01", align_bytes=64, offset=STEP * 3)
+            nc.vector.quantize_mx(out=codes[:].bitcast(FP8X4), scales=scales[:], in_=hbs["pair"][:].rearrange("p e g n t -> p (e g n t)"))
+            for e in range(2):
+                hc[e] = codes[:, e * 2 * C:(e + 1) * 2 * C]
+                hs[e] = scales[:, e * 2 * C:(e + 1) * 2 * C]
+
         def h_quant(e):
-            hc[e] = keep.tile([P, 2 * C], U32, name="hc%d" % e, align_bytes=64)
-            hs[e] = arena.tile([P, 2 * C], U8, name="hs%d" % e, align_bytes=64, offset=STEP * (2 + e))
-            nc.vector.quantize_mx(out=hc[e][:].bitcast(FP8X4), scales=hs[e][:], in_=hbs[e][:].rearrange("p g n t -> p (g n t)"))
+            codes = keep.tile([P, 2 * C], U32, name="hc%d" % e, align_bytes=64)
+            scales = arena.tile([P, 2 * C], U8, name="hs%d" % e, align_bytes=64, offset=STEP * (3 + e))
+            nc.vector.quantize_mx(out=codes[:].bitcast(FP8X4), scales=scales[:], in_=hbs[e][:].rearrange("p g n t -> p (g n t)"))
+            hc[e] = codes[:]
+            hs[e] = scales[:]
 
         def l2_pass(acc, e, g, m):
             cols = slice(g * N + m * P, g * N + (m + 1) * P)
@@ -231,20 +250,17 @@ def tile_routed_moe_kernel(tc, xT, w1, w2, gate, offs, pos1, pos2, out):
         x_gather()
         w1_path(0)
         x_path(0)
-        x_path(1)
         load_w2(2)
         layer1(0)
         w1_path(1)
-        x_path(2)
-        x_path(3)
+        x_path(1)
         load_w2(3)
         layer1(1)
         w1_path(2)
-        h_quant(0)
         load_gates()
         layer1(2)
         w1_path(3)
-        h_quant(1)
+        h_quant_first()
         layer1(3)
         for e in range(E - 1):
             w2_path(e)
@@ -254,7 +270,7 @@ def tile_routed_moe_kernel(tc, xT, w1, w2, gate, offs, pos1, pos2, out):
                 layer2(e, m)
         e = E - 1
         w2_tiles(e)
-        chunk_offset = (STEP * 7, STEP * 7 + 2048, STEP * 7 + 4096, STEP * 7)
+        chunk_offset = (STEP * 8, STEP * 8 + 2048, STEP * 8 + 4096, STEP * 8)
         for m in range(4):
             gc = arena.tile([P, 2, P, 4], BF16, name="gc%d" % m, align_bytes=64, offset=chunk_offset[m])
             copy_on(

@@ -237,6 +237,14 @@ def tile_routed_moe_kernel(tc, xT, w1, w2, gate, offs, pos1, pos2, out):
             b = fin.tile([P, T], F32, name="prod_b")
             o = fin.tile([P, T], F32, name="res")
             nc.vector.tensor_tensor(a[:], y[m][:].indirect(pos1_t[:]), gates[m][:, 0, :], MULT)
+            if m >= PE_ADD:
+                half = T // 2
+                for i in range(2):
+                    cols = slice(i * half, (i + 1) * half)
+                    nc.vector.tensor_tensor(b[:, cols], y[m][:].indirect(pos2_t[:, i * (half // 16):(i + 1) * (half // 16)]), gates[m][:, 1, cols], MULT)
+                    nc.vector.tensor_tensor(o[:, cols], a[:, cols], b[:, cols], ADD)
+                    nc.sync.dma_start(out[m * P:(m + 1) * P, cols], o[:, cols])
+                return
             nc.vector.tensor_tensor(b[:], y[m][:].indirect(pos2_t[:]), gates[m][:, 1, :], MULT)
             if m < PE_ADD:
                 total = ps1.tile([P, T], F32, name="acc1")

@@ -24,7 +24,6 @@ X_FORM = ("f", "f", "a", "a")
 W1_PIECES = (1, 1, 1, 1)
 ENG_W1 = (("v", "v"), ("v", "v"), ("v", "v"), ("v", "v"))
 ENG_W2 = (("s", "v"), ("s", "v"), ("s", "v"))
-ENG_LAST = ("v", "s", "s", "v")
 ENG_Y = ("s", "s")
 PE_ADD = 3
 
@@ -160,7 +159,10 @@ def tile_routed_moe_kernel(tc, xT, w1, w2, gate, offs, pos1, pos2, out):
 
         def w2_path(e):
             w2_tiles(e)
-            gb = arena.tile([P, 2, N, 4], BF16, name="gb%d" % (4 + e), align_bytes=64, offset=STEP * (5 + e))
+            if e == 1:
+                gb = hfirst.tile([P, 2, N, 4], BF16, name="gb5", align_bytes=64, offset=0)
+            else:
+                gb = arena.tile([P, 2, N, 4], BF16, name="gb%d" % (4 + e), align_bytes=64, offset=STEP * (5 + e))
             if ENG_W2[e][0] == ENG_W2[e][1]:
                 copy_on(ENG_W2[e][0], gb[:].rearrange("p g (c i) j -> p g c j i", i=4), raw_w2[e][:].rearrange("p g j (c i) -> p g c j i", i=4))
             else:
@@ -170,7 +172,7 @@ def tile_routed_moe_kernel(tc, xT, w1, w2, gate, offs, pos1, pos2, out):
 
         def layer1(e):
             if e == 0:
-                hbs["pair"] = hfirst.tile([P, 2, 2, C, 4], BF16, name="hpair", align_bytes=64)
+                hbs["pair"] = hfirst.tile([P, 2, 2, C, 4], BF16, name="hpair", align_bytes=64, offset=0)
             if e < 2:
                 hb = hbs["pair"][:, e]
             else:
@@ -202,7 +204,10 @@ def tile_routed_moe_kernel(tc, xT, w1, w2, gate, offs, pos1, pos2, out):
 
         def h_quant(e):
             codes = keep.tile([P, 2 * C], U32, name="hc%d" % e, align_bytes=64)
-            scales = arena.tile([P, 2 * C], U8, name="hs%d" % e, align_bytes=64, offset=STEP * (3 + e))
+            if e == 2:
+                scales = arena.tile([P, 2 * C], U8, name="hs2", align_bytes=64, offset=STEP * 5)
+            else:
+                scales = hfirst.tile([P, 2 * C], U8, name="hs3", align_bytes=64, offset=0)
             nc.vector.quantize_mx(out=codes[:].bitcast(FP8X4), scales=scales[:], in_=hbs[e][:].rearrange("p g n t -> p (g n t)"))
             hc[e] = codes[:]
             hs[e] = scales[:]
@@ -278,30 +283,42 @@ def tile_routed_moe_kernel(tc, xT, w1, w2, gate, offs, pos1, pos2, out):
                 layer2(e, m)
         e = E - 1
         w2_tiles(e)
-        chunk_offset = (STEP * 8, STEP * 8 + 2048, STEP * 8 + 4096, STEP * 8)
-        for m in range(4):
-            gc = arena.tile([P, 2, P, 4], BF16, name="gc%d" % m, align_bytes=64, offset=chunk_offset[m])
+        half = N // 2
+
+        def last_copy(engine, tile, g, c0):
             copy_on(
-                ENG_LAST[m],
-                gc[:].rearrange("p g (c i) j -> p g c j i", i=4),
-                raw_w2[e][:, :, :, m * P:(m + 1) * P].rearrange("p g j (c i) -> p g c j i", i=4),
+                engine,
+                tile[:].rearrange("p (c i) j -> p c j i", i=4),
+                raw_w2[e][:, g, :, c0:c0 + half].rearrange("p j (c i) -> p c j i", i=4),
             )
+
+        def last_quant(tile, g, c0):
+            first = g * N + c0
             nc.vector.quantize_mx(
-                out=w2c[e][:, m * 2 * P:(m + 1) * 2 * P].bitcast(FP8X4),
-                scales=w2s[e][:, m * 2 * P:(m + 1) * 2 * P],
-                in_=gc[:].rearrange("p g n j -> p (g n j)"),
+                out=w2c[e][:, first:first + half].bitcast(FP8X4),
+                scales=w2s[e][:, first:first + half],
+                in_=tile[:].rearrange("p n j -> p (n j)"),
             )
+
+        q00 = hfirst.tile([P, half, 4], BF16, name="q00", align_bytes=64, offset=4096)
+        last_copy("s", q00, 0, 0)
+        q10 = arena.tile([P, half, 4], BF16, name="q10", align_bytes=64, offset=STEP * 8)
+        last_copy("v", q10, 1, 0)
+        last_quant(q00, 0, 0)
+        last_quant(q10, 1, 0)
+        for m in range(2):
             for g in range(2):
-                cols = slice((m * 2 + g) * P, (m * 2 + g + 1) * P)
-                nc.tensor.matmul_mx(
-                    out=banks[m][:, 1, :],
-                    lhsT=w2c[e][:, cols].bitcast(FP8X4),
-                    lhsT_scale=w2s[e][:, cols],
-                    rhs=hc[e][:, g * C:(g + 1) * C].bitcast(FP8X4),
-                    rhs_scale=hs[e][:, g * C:(g + 1) * C],
-                    start=(g == 0),
-                    stop=(g == 1),
-                )
+                l2_pass(banks[m][:, 1, :], e, g, m)
+            evacuate(e, m)
+        q01 = arena.tile([P, half, 4], BF16, name="q01", align_bytes=64, offset=STEP * 8)
+        last_copy("v", q01, 0, half)
+        q11 = hfirst.tile([P, half, 4], BF16, name="q11", align_bytes=64, offset=4096)
+        last_copy("v", q11, 1, half)
+        last_quant(q01, 0, half)
+        last_quant(q11, 1, half)
+        for m in range(2, 4):
+            for g in range(2):
+                l2_pass(banks[m][:, 1, :], e, g, m)
             evacuate(e, m)
         for m in range(4):
             combine(m)

@@ -18,13 +18,11 @@ MULT = mybir.AluOpType.mult
 ADD = mybir.AluOpType.add
 
 P = 128
-RAW_BUFS = 6
+RAW_BUFS = 5
 STEP = 512
 X_FORM = ("f", "f", "a", "a")
 W1_PIECES = (1, 1, 1, 1)
 ENG_W1 = (("v", "v"), ("v", "v"), ("v", "v"), ("v", "v"))
-ENG_W2 = (("s", "v"), ("s", "v"), ("s", "v"))
-ENG_Y = ("s", "s")
 PE_ADD = 3
 
 
@@ -44,9 +42,11 @@ def tile_routed_moe_kernel(tc, xT, w1, w2, gate, offs, pos1, pos2, out):
         arena = ctx.enter_context(tc.tile_pool(name="arena", bufs=1))
         xstage = ctx.enter_context(tc.tile_pool(name="xstage", bufs=2))
         xbpool = ctx.enter_context(tc.tile_pool(name="xbpool", bufs=2))
-        hstage = ctx.enter_context(tc.tile_pool(name="hstage", bufs=2))
+        hstage = ctx.enter_context(tc.tile_pool(name="hstage", bufs=1))
+        shared = ctx.enter_context(tc.tile_pool(name="shared", bufs=1))
         hfirst = ctx.enter_context(tc.tile_pool(name="hfirst", bufs=1))
         fin = ctx.enter_context(tc.tile_pool(name="fin", bufs=2))
+        results = ctx.enter_context(tc.tile_pool(name="results", bufs=4))
         ps1 = ctx.enter_context(tc.psum_pool(name="ps1", bufs=4))
         ps2 = ctx.enter_context(tc.psum_pool(name="ps2", bufs=4))
 
@@ -81,21 +81,32 @@ def tile_routed_moe_kernel(tc, xT, w1, w2, gate, offs, pos1, pos2, out):
             raw_w1[e] = r
 
         def load_w2(e):
-            r = raw.tile([P, 2, 4, N], F32, name="rawt")
-            for g in range(2):
-                src = w2[e][g * 512:(g + 1) * 512, :].rearrange("(p j) n -> p j n", j=4)
-                if e == E - 1 and g == 1:
-                    for m in range(2):
-                        nc.sync.dma_start(r[:, g, :, m * 2 * P:(m + 1) * 2 * P], src[:, :, m * 2 * P:(m + 1) * 2 * P])
-                else:
-                    nc.sync.dma_start(r[:, g], src)
-            raw_w2[e] = r
+            if e == 1:
+                parts = [shared.tile([P, 4, N], F32, name="raw_w2_1_%d" % g, align_bytes=64, offset=8192 * g)[:] for g in range(2)]
+            else:
+                r = raw.tile([P, 2, 4, N], F32, name="rawt")
+                parts = [r[:, g] for g in range(2)]
+            raw_w2[e] = parts
+            if e < E - 1:
+                for g in range(2):
+                    nc.sync.dma_start(parts[g], w2[e][g * 512:(g + 1) * 512, :].rearrange("(p j) n -> p j n", j=4))
 
-        def load_gates():
-            r = raw.tile([P, 4, 2, T], F32, name="rawt")
-            for m in range(4):
-                nc.sync.dma_start(r[:, m], gate[:, m * P:(m + 1) * P, :].rearrange("r p t -> p r t"))
-                gates[m] = r[:, m]
+        def load_last_half(half):
+            cols = slice(half * 2 * P, (half + 1) * 2 * P)
+            for g in range(2):
+                src = w2[E - 1][g * 512:(g + 1) * 512, :].rearrange("(p j) n -> p j n", j=4)
+                nc.sync.dma_start(raw_w2[E - 1][g][:, :, cols], src[:, :, cols])
+
+        def load_gates(first, last):
+            for m in range(first, last):
+                nc.sync.dma_start(gates["tile"][:, m], gate[:, m * P:(m + 1) * P, :].rearrange("r p t -> p r t"))
+                gates[m] = gates["tile"][:, m]
+
+        def load_first_gate(r):
+            if r == 0:
+                gates["tile"] = raw.tile([P, 4, 2, T], F32, name="rawt")
+                gates[0] = gates["tile"][:, 0]
+            nc.sync.dma_start(gates[0][:, r, :], gate[r, 0:P, :])
 
         load_w1(0, 1)
         load_w1(1, 1)
@@ -109,7 +120,7 @@ def tile_routed_moe_kernel(tc, xT, w1, w2, gate, offs, pos1, pos2, out):
         load_w2(1)
 
         xc, xs, w1c, w1s, w2c, w2s, hc, hs = {}, {}, {}, {}, {}, {}, {}, {}
-        y = [keep.tile([P, E * C], F32, name="y%d" % m) for m in range(4)]
+        y = {}
 
         xbs = {}
         xpair = {}
@@ -157,26 +168,52 @@ def tile_routed_moe_kernel(tc, xT, w1, w2, gate, offs, pos1, pos2, out):
             w2c[e] = keep.tile([P, 2 * N], U32, name="w2c%d" % e, align_bytes=64)
             w2s[e] = keep.tile([P, 2 * N], U8, name="w2s%d" % e, align_bytes=64)
 
+        def w2_copy(engine, dst, e, g, c0, width):
+            copy_on(
+                engine,
+                dst.rearrange("p (c i) j -> p c j i", i=4),
+                raw_w2[e][g][:, :, c0:c0 + width].rearrange("p j (c i) -> p c j i", i=4),
+            )
+
+        def w2_quant(tile, e, first, width):
+            nc.vector.quantize_mx(
+                out=w2c[e][:, first:first + width].bitcast(FP8X4),
+                scales=w2s[e][:, first:first + width],
+                in_=tile[:].rearrange("p g n j -> p (g n j)"),
+            )
+
+        HALF = N // 2
+
+        def w2_columns(e, g, m):
+            first = g * N + m * P if e < 2 else (m // 2) * N + g * HALF + (m % 2) * P
+            return slice(first, first + P)
+
         def w2_path(e):
             w2_tiles(e)
-            if e == 1:
-                gb = hfirst.tile([P, 2, N, 4], BF16, name="gb5", align_bytes=64, offset=0)
+            if e == 0:
+                gb = arena.tile([P, 2, N, 4], BF16, name="gb0_2", align_bytes=64, offset=STEP * 5)
             else:
-                gb = arena.tile([P, 2, N, 4], BF16, name="gb%d" % (4 + e), align_bytes=64, offset=STEP * (5 + e))
-            if ENG_W2[e][0] == ENG_W2[e][1]:
-                copy_on(ENG_W2[e][0], gb[:].rearrange("p g (c i) j -> p g c j i", i=4), raw_w2[e][:].rearrange("p g j (c i) -> p g c j i", i=4))
-            else:
-                for g in range(2):
-                    copy_on(ENG_W2[e][g], gb[:, g].rearrange("p (c i) j -> p c j i", i=4), raw_w2[e][:, g].rearrange("p j (c i) -> p c j i", i=4))
-            nc.vector.quantize_mx(out=w2c[e][:].bitcast(FP8X4), scales=w2s[e][:], in_=gb[:].rearrange("p g n j -> p (g n j)"))
+                gb = hfirst.tile([P, 2, N, 4], BF16, name="gb1_2", align_bytes=64, offset=0)
+            w2_copy("s", gb[:, 0], e, 0, 0, N)
+            w2_copy("v", gb[:, 1], e, 1, 0, N)
+            w2_quant(gb, e, 0, 2 * N)
+
+        def w2_halves(e, pool, first, engines):
+            w2_tiles(e)
+            tiles = [pool.tile([P, 2, HALF, 4], BF16, name="half%d_%d" % (e, h), align_bytes=64, offset=first + 4096 * h) for h in range(2)]
+            for g, h, engine in engines:
+                w2_copy(engine, tiles[h][:, g], e, g, h * HALF, HALF)
+            return tiles
 
         def layer1(e):
             if e == 0:
                 hbs["pair"] = hfirst.tile([P, 2, 2, C, 4], BF16, name="hpair", align_bytes=64, offset=0)
             if e < 2:
                 hb = hbs["pair"][:, e]
-            else:
+            elif e == 2:
                 hb = hstage.tile([P, 2, C, 4], BF16, name="hb", align_bytes=64)
+            else:
+                hb = shared.tile([P, 2, C, 4], BF16, name="hb3", align_bytes=64, offset=0)
             for g2 in range(2):
                 for s in range(2):
                     acc = ps1.tile([P, 4, P], F32, name="acc1")
@@ -207,13 +244,13 @@ def tile_routed_moe_kernel(tc, xT, w1, w2, gate, offs, pos1, pos2, out):
             if e == 2:
                 scales = arena.tile([P, 2 * C], U8, name="hs2", align_bytes=64, offset=STEP * 5)
             else:
-                scales = hfirst.tile([P, 2 * C], U8, name="hs3", align_bytes=64, offset=0)
+                scales = shared.tile([P, 2 * C], U8, name="hs3", align_bytes=64, offset=8192)
             nc.vector.quantize_mx(out=codes[:].bitcast(FP8X4), scales=scales[:], in_=hbs[e][:].rearrange("p g n t -> p (g n t)"))
             hc[e] = codes[:]
             hs[e] = scales[:]
 
         def l2_pass(acc, e, g, m):
-            cols = slice(g * N + m * P, g * N + (m + 1) * P)
+            cols = w2_columns(e, g, m)
             nc.tensor.matmul_mx(
                 out=acc,
                 lhsT=w2c[e][:, cols].bitcast(FP8X4),
@@ -227,20 +264,29 @@ def tile_routed_moe_kernel(tc, xT, w1, w2, gate, offs, pos1, pos2, out):
         banks = {}
 
         def layer2(e, m):
-            if e % 2 == 0:
+            if e == 0:
                 banks[m] = ps2.tile([P, 2, C], F32, name="acc2")
+            elif e == 2:
+                late_banks[m] = ps1.tile([P, 2, C], F32, name="acc1")
             for g in range(2):
-                l2_pass(banks[m][:, e % 2, :], e, g, m)
-            if e % 2 == 1:
-                evacuate(e, m)
+                l2_pass((banks if e < 2 else late_banks)[m][:, e % 2, :], e, g, m)
 
-        def evacuate(e, m):
-            copy_on(ENG_Y[e // 2], y[m][:, (e - 1) * C:(e + 1) * C], banks[m][:].rearrange("p a c -> p (a c)"))
+        late_banks = {}
+
+        def evacuate(m, pair):
+            if pair == 0:
+                pool, offset = ((arena, STEP * 6), (arena, STEP * 6 + 4096), (hfirst, 0), (hfirst, 4096))[m]
+                y[m] = pool.tile([P, E * C], F32, name="y%d" % m, align_bytes=64, offset=offset)
+            bank = (banks, late_banks)[pair][m]
+            copy_on("s", y[m][:, pair * 2 * C:(pair + 1) * 2 * C], bank[:].rearrange("p a c -> p (a c)"))
+
+        def evacuate_first(e):
+            copy_on("s", y[0][:, e * C:(e + 1) * C], late_banks[0][:, e - 2, :])
 
         def combine(m):
             a = fin.tile([P, T], F32, name="prod_a")
             b = fin.tile([P, T], F32, name="prod_b")
-            o = fin.tile([P, T], F32, name="res")
+            o = results.tile([P, T], F32, name="res")
             nc.vector.tensor_tensor(a[:], y[m][:].indirect(pos1_t[:]), gates[m][:, 0, :], MULT)
             if m >= PE_ADD:
                 half = T // 2
@@ -251,14 +297,15 @@ def tile_routed_moe_kernel(tc, xT, w1, w2, gate, offs, pos1, pos2, out):
                     nc.sync.dma_start(out[m * P:(m + 1) * P, cols], o[:, cols])
                 return
             nc.vector.tensor_tensor(b[:], y[m][:].indirect(pos2_t[:]), gates[m][:, 1, :], MULT)
-            if m < PE_ADD:
-                total = ps1.tile([P, T], F32, name="acc1")
-                nc.tensor.matmul(out=total[:], lhsT=ident[:], rhs=a[:], start=True, stop=False)
-                nc.tensor.matmul(out=total[:], lhsT=ident[:], rhs=b[:], start=False, stop=True)
-                nc.scalar.copy(out=o[:], in_=total[:])
-            else:
-                nc.vector.tensor_tensor(o[:], a[:], b[:], ADD)
-            nc.sync.dma_start(out[m * P:(m + 1) * P, :], o[:])
+            parts = 2 if m == PE_ADD - 1 else 1
+            spans = [slice(i * T // parts, (i + 1) * T // parts) for i in range(parts)]
+            totals = [ps2.tile([P, T // parts], F32, name="acc2") for cols in spans]
+            for prod in (a, b):
+                for total, cols in zip(totals, spans):
+                    nc.tensor.matmul(out=total[:], lhsT=ident[:], rhs=prod[:, cols], start=prod is a, stop=prod is b)
+            for total, cols in zip(totals, spans):
+                nc.scalar.copy(out=o[:, cols], in_=total[:])
+                nc.sync.dma_start(out[m * P:(m + 1) * P, cols], o[:, cols])
 
         x_gather()
         w1_path(0)
@@ -268,57 +315,39 @@ def tile_routed_moe_kernel(tc, xT, w1, w2, gate, offs, pos1, pos2, out):
         w1_path(1)
         x_path(1)
         load_w2(3)
+        load_last_half(0)
         layer1(1)
         w1_path(2)
-        load_gates()
+        load_first_gate(0)
+        load_last_half(1)
+        load_first_gate(1)
+        load_gates(1, 4)
         layer1(2)
         w1_path(3)
         h_quant_first()
         layer1(3)
-        for e in range(E - 1):
+        for e in range(2):
             w2_path(e)
-            if e < 2:
-                h_quant(2 + e)
+            h_quant(2 + e)
             for m in range(4):
                 layer2(e, m)
-        e = E - 1
-        w2_tiles(e)
-        half = N // 2
-
-        def last_copy(engine, tile, g, c0):
-            copy_on(
-                engine,
-                tile[:].rearrange("p (c i) j -> p c j i", i=4),
-                raw_w2[e][:, g, :, c0:c0 + half].rearrange("p j (c i) -> p c j i", i=4),
-            )
-
-        def last_quant(tile, g, c0):
-            first = g * N + c0
-            nc.vector.quantize_mx(
-                out=w2c[e][:, first:first + half].bitcast(FP8X4),
-                scales=w2s[e][:, first:first + half],
-                in_=tile[:].rearrange("p n j -> p (n j)"),
-            )
-
-        q00 = hfirst.tile([P, half, 4], BF16, name="q00", align_bytes=64, offset=4096)
-        last_copy("s", q00, 0, 0)
-        q10 = arena.tile([P, half, 4], BF16, name="q10", align_bytes=64, offset=STEP * 8)
-        last_copy("v", q10, 1, 0)
-        last_quant(q00, 0, 0)
-        last_quant(q10, 1, 0)
-        for m in range(2):
-            for g in range(2):
-                l2_pass(banks[m][:, 1, :], e, g, m)
-            evacuate(e, m)
-        q01 = arena.tile([P, half, 4], BF16, name="q01", align_bytes=64, offset=STEP * 8)
-        last_copy("v", q01, 0, half)
-        q11 = hfirst.tile([P, half, 4], BF16, name="q11", align_bytes=64, offset=4096)
-        last_copy("v", q11, 1, half)
-        last_quant(q01, 0, half)
-        last_quant(q11, 1, half)
-        for m in range(2, 4):
-            for g in range(2):
-                l2_pass(banks[m][:, 1, :], e, g, m)
-            evacuate(e, m)
+        tiles = w2_halves(2, arena, STEP * 6, ((0, 0, "s"), (0, 1, "s"), (1, 0, "v"), (1, 1, "s")))
+        for h in range(2):
+            w2_quant(tiles[h], 2, h * N, N)
+            for m in (2 * h, 2 * h + 1):
+                layer2(2, m)
+                if m == 0:
+                    evacuate(0, 0)
+                    evacuate_first(2)
+        tiles = w2_halves(3, hfirst, 0, ((0, 0, "s"), (1, 0, "v"), (0, 1, "v"), (1, 1, "s")))
+        for h in range(2):
+            w2_quant(tiles[h], 3, h * N, N)
+            for m in (2 * h, 2 * h + 1):
+                layer2(3, m)
+                if m == 0:
+                    evacuate_first(3)
+                else:
+                    evacuate(m, 0)
+                    evacuate(m, 1)
         for m in range(4):
             combine(m)

@@ -70,6 +70,8 @@ def tile_routed_moe_kernel(tc, xT, w1, w2, gate, offs, pos1, pos2, out):
 
         raw_w1 = {}
         raw_w2 = {}
+        raw_whole = {}
+        blocks = []
         gates = {}
 
         def load_w1(e, pieces):
@@ -86,6 +88,7 @@ def tile_routed_moe_kernel(tc, xT, w1, w2, gate, offs, pos1, pos2, out):
             else:
                 r = raw.tile([P, 2, 4, N], F32, name="rawt")
                 parts = [r[:, g] for g in range(2)]
+                raw_whole[e] = r
             raw_w2[e] = parts
             if e < E - 1:
                 for g in range(2):
@@ -185,7 +188,12 @@ def tile_routed_moe_kernel(tc, xT, w1, w2, gate, offs, pos1, pos2, out):
         HALF = N // 2
 
         def w2_columns(e, g, m):
-            first = g * N + m * P if e < 2 else (m // 2) * N + g * HALF + (m % 2) * P
+            if e < 2:
+                first = g * N + m * P
+            elif e == 3 and m < 2:
+                first = m * 2 * P + g * P
+            else:
+                first = (m // 2) * N + g * HALF + (m % 2) * P
             return slice(first, first + P)
 
         def w2_path(e):
@@ -275,7 +283,7 @@ def tile_routed_moe_kernel(tc, xT, w1, w2, gate, offs, pos1, pos2, out):
 
         def evacuate(m, pair):
             if pair == 0:
-                pool, offset = ((arena, STEP * 6), (arena, STEP * 6 + 4096), (hfirst, 0), (hfirst, 4096))[m]
+                pool, offset = ((arena, STEP * 6), (arena, STEP * 6 + 4096), (hfirst, 4096), (shared, 8192))[m]
                 y[m] = pool.tile([P, E * C], F32, name="y%d" % m, align_bytes=64, offset=offset)
             bank = (banks, late_banks)[pair][m]
             copy_on("s", y[m][:, pair * 2 * C:(pair + 1) * 2 * C], bank[:].rearrange("p a c -> p (a c)"))
@@ -339,15 +347,30 @@ def tile_routed_moe_kernel(tc, xT, w1, w2, gate, offs, pos1, pos2, out):
                 if m == 0:
                     evacuate(0, 0)
                     evacuate_first(2)
-        tiles = w2_halves(3, hfirst, 0, ((0, 0, "s"), (1, 0, "v"), (0, 1, "v"), (1, 1, "s")))
-        for h in range(2):
-            w2_quant(tiles[h], 3, h * N, N)
-            for m in (2 * h, 2 * h + 1):
-                layer2(3, m)
-                if m == 0:
-                    evacuate_first(3)
-                else:
-                    evacuate(m, 0)
-                    evacuate(m, 1)
+        w2_tiles(3)
+        for m in range(2):
+            block = hfirst.tile([P, 2, P, 4], BF16, name="block%d" % m, align_bytes=64, offset=2048 * m)
+            copy_on(
+                "v",
+                block[:].rearrange("p g (c i) j -> p g c j i", i=4),
+                raw_whole[3][:, :, :, m * P:(m + 1) * P].rearrange("p g j (c i) -> p g c j i", i=4),
+            )
+            blocks.append(block)
+        second = hfirst.tile([P, 2, HALF, 4], BF16, name="second", align_bytes=64, offset=4096)
+        w2_copy("v", second[:, 0], 3, 0, HALF, HALF)
+        w2_copy("s", second[:, 1], 3, 1, HALF, HALF)
+        for m in range(2):
+            w2_quant(blocks[m], 3, m * 2 * P, 2 * P)
+            layer2(3, m)
+            if m == 0:
+                evacuate_first(3)
+            else:
+                evacuate(m, 0)
+                evacuate(m, 1)
+        w2_quant(second, 3, N, N)
+        for m in (2, 3):
+            layer2(3, m)
+            evacuate(m, 0)
+            evacuate(m, 1)
         for m in range(4):
             combine(m)

from contextlib import ExitStack

import concourse.mybir as mybir
from concourse.masks import make_identity

K, T, E, C, H, N = 512, 512, 4, 256, 1024, 512
FLOPS = 2 * E * C * (K * H + H * N)

F32 = mybir.dt.float32
BF16 = mybir.dt.bfloat16
U32 = mybir.dt.uint32
U16 = mybir.dt.uint16
U8 = mybir.dt.uint8
FP8X4 = mybir.dt.float8_e4m3fn_x4
GELU = mybir.ActivationFunctionType.Gelu_apprx_tanh
COPY = mybir.ActivationFunctionType.Copy
MULT = mybir.AluOpType.mult
ADD = mybir.AluOpType.add

P = 128
RAW_BUFS = 5
STEP = 512
X_FORM = ("f", "f", "a", "a")
W1_PIECES = (1, 1, 1, 1)
ENG_W1 = (("v", "v"), ("v", "v"), ("v", "v"), ("v", "v"))
PE_ADD = 3


def tile_routed_moe_kernel(tc, xT, w1, w2, gate, offs, pos1, pos2, out):
    nc = tc.nc

    def copy_on(engine, dst, src):
        if engine == "v":
            nc.vector.tensor_copy(out=dst, in_=src)
        else:
            nc.scalar.copy(out=dst, in_=src)

    with ExitStack() as ctx:
        lists = ctx.enter_context(tc.tile_pool(name="lists", bufs=1))
        keep = ctx.enter_context(tc.tile_pool(name="keep", bufs=1))
        raw = ctx.enter_context(tc.tile_pool(name="raw", bufs=RAW_BUFS))
        arena = ctx.enter_context(tc.tile_pool(name="arena", bufs=1))
        xstage = ctx.enter_context(tc.tile_pool(name="xstage", bufs=2))
        xbpool = ctx.enter_context(tc.tile_pool(name="xbpool", bufs=2))
        hstage = ctx.enter_context(tc.tile_pool(name="hstage", bufs=1))
        shared = ctx.enter_context(tc.tile_pool(name="shared", bufs=1))
        hfirst = ctx.enter_context(tc.tile_pool(name="hfirst", bufs=1))
        fin = ctx.enter_context(tc.tile_pool(name="fin", bufs=2))
        results = ctx.enter_context(tc.tile_pool(name="results", bufs=4))
        ps1 = ctx.enter_context(tc.psum_pool(name="ps1", bufs=4))
        ps2 = ctx.enter_context(tc.psum_pool(name="ps2", bufs=4))

        warm_in = keep.tile([P, 8], F32, name="warm_in")
        warm_out = keep.tile([P, 8], F32, name="warm_out")
        nc.gpsimd.memset(warm_in[:], 0.0)
        nc.scalar.activation(out=warm_out[:], in_=warm_in[:], func=GELU)

        ident = keep.tile([P, P], F32, name="ident")
        make_identity(nc, ident[:])

        offs_t = lists.tile([P, E * C // 16], U16, name="offs_t")
        nc.sync.dma_start(offs_t[:], offs)
        x_view = xT.rearrange("(p t) n -> p t n", t=4)
        plane0 = keep.tile([P, T], F32, name="plane0")
        nc.sync.dma_start(plane0[:], x_view[:, 0, :])
        rest = keep.tile([P, 3, T], F32, name="planes123")
        nc.sync.dma_start(rest[:], x_view[:, 1:4, :])
        planes = [plane0[:]] + [rest[:, t, :] for t in range(3)]
        xbf = keep.tile([P, 4, T], BF16, name="xbf")

        raw_w1 = {}
        raw_w2 = {}
        raw_whole = {}
        blocks = []
        gates = {}

        def load_w1(e, pieces):
            r = raw.tile([P, 4, H], F32, name="rawt")
            src = w1[e].rearrange("(p j) c -> p j c", j=4)
            width = H // pieces
            for i in range(pieces):
                nc.sync.dma_start(r[:, :, i * width:(i + 1) * width], src[:, :, i * width:(i + 1) * width])
            raw_w1[e] = r

        def load_w2(e):
            if e == 1:
                parts = [shared.tile([P, 4, N], F32, name="raw_w2_1_%d" % g, align_bytes=64, offset=8192 * g)[:] for g in range(2)]
            else:
                r = raw.tile([P, 2, 4, N], F32, name="rawt")
                parts = [r[:, g] for g in range(2)]
                raw_whole[e] = r
            raw_w2[e] = parts
            if e < E - 1:
                for g in range(2):
                    nc.sync.dma_start(parts[g], w2[e][g * 512:(g + 1) * 512, :].rearrange("(p j) n -> p j n", j=4))

        def load_last_half(half):
            cols = slice(half * 2 * P, (half + 1) * 2 * P)
            for g in range(2):
                src = w2[E - 1][g * 512:(g + 1) * 512, :].rearrange("(p j) n -> p j n", j=4)
                nc.sync.dma_start(raw_w2[E - 1][g][:, :, cols], src[:, :, cols])

        def load_gates(first, last):
            for m in range(first, last):
                nc.sync.dma_start(gates["tile"][:, m], gate[:, m * P:(m + 1) * P, :].rearrange("r p t -> p r t"))
                gates[m] = gates["tile"][:, m]

        def load_first_gate(r):
            if r == 0:
                gates["tile"] = raw.tile([P, 4, 2, T], F32, name="rawt")
                gates[0] = gates["tile"][:, 0]
            nc.sync.dma_start(gates[0][:, r, :], gate[r, 0:P, :])

        load_w1(0, 1)
        load_w1(1, 1)
        pos1_t = lists.tile([P, T // 16], U16, name="pos1_t")
        nc.sync.dma_start(pos1_t[:], pos1)
        pos2_t = lists.tile([P, T // 16], U16, name="pos2_t")
        nc.sync.dma_start(pos2_t[:], pos2)
        load_w1(2, 1)
        load_w1(3, 1)
        load_w2(0)
        load_w2(1)

        xc, xs, w1c, w1s, w2c, w2s, hc, hs = {}, {}, {}, {}, {}, {}, {}, {}
        y = {}

        xbs = {}
        xpair = {}
        g4s = {}
        hbs = {}

        def x_gather():
            for q in range(2):
                xpair[q] = xbpool.tile([P, 2 * C, 4], BF16, name="xb", align_bytes=64)
            for e in range(E):
                xbs[e] = xpair[e // 2][:, (e % 2) * C:(e % 2 + 1) * C, :]
                if X_FORM[e] == "a":
                    g4s[e] = xstage.tile([P, 4, C], F32, name="g4")
            for t in range(4):
                nc.vector.tensor_copy(out=xbf[:, t, :], in_=planes[t])
                for e in range(E):
                    slots = offs_t[:, e * (C // 16):(e + 1) * (C // 16)]
                    if X_FORM[e] == "a":
                        nc.vector.tensor_copy(g4s[e][:, t, :], planes[t].indirect(slots))
                    else:
                        nc.scalar.activation(out=xbs[e][:, :, t], in_=xbf[:, t, :].indirect(slots), func=COPY)

        def x_path(q):
            for e in (2 * q, 2 * q + 1):
                if X_FORM[e] == "a":
                    copy_on("s", xbs[e].rearrange("p (c i) t -> p c t i", i=4), g4s[e][:].rearrange("p t (c i) -> p c t i", i=4))
            xc[q] = keep.tile([P, 2 * C], U32, name="xc%d" % q, align_bytes=64)
            xs[q] = arena.tile([P, 2 * C], U8, name="xs%d" % q, align_bytes=64, offset=2 * C * q)
            nc.vector.quantize_mx(out=xc[q][:].bitcast(FP8X4), scales=xs[q][:], in_=xpair[q][:].rearrange("p n t -> p (n t)"))

        def w1_path(e):
            w1c[e] = keep.tile([P, H], U32, name="w1c%d" % e, align_bytes=64)
            w1s[e] = keep.tile([P, H], U8, name="w1s%d" % e, align_bytes=64)
            gb = arena.tile([P, 4, 2 * P, 4], BF16, name="gb%d" % e, align_bytes=64, offset=STEP * e)
            spans = ((0, 2 * P),) if W1_PIECES[e] == 1 else ((0, P), (P, 2 * P))
            for q0, q1 in spans:
                copy_on(
                    ENG_W1[e][q0 // P],
                    gb[:, :, q0:q1, :].rearrange("p t q j -> p q j t"),
                    raw_w1[e][:, :, 4 * q0:4 * q1].rearrange("p j (q t) -> p q j t", t=4),
                )
            nc.vector.quantize_mx(out=w1c[e][:].bitcast(FP8X4), scales=w1s[e][:], in_=gb[:].rearrange("p t q j -> p (t q j)"))

        def w2_tiles(e):
            w2c[e] = keep.tile([P, 2 * N], U32, name="w2c%d" % e, align_bytes=64)
            w2s[e] = keep.tile([P, 2 * N], U8, name="w2s%d" % e, align_bytes=64)

        def w2_copy(engine, dst, e, g, c0, width):
            copy_on(
                engine,
                dst.rearrange("p (c i) j -> p c j i", i=4),
                raw_w2[e][g][:, :, c0:c0 + width].rearrange("p j (c i) -> p c j i", i=4),
            )

        def w2_quant(tile, e, first, width):
            nc.vector.quantize_mx(
                out=w2c[e][:, first:first + width].bitcast(FP8X4),
                scales=w2s[e][:, first:first + width],
                in_=tile[:].rearrange("p g n j -> p (g n j)"),
            )

        HALF = N // 2

        def w2_columns(e, g, m):
            if e < 2:
                first = g * N + m * P
            elif e == 3 and m < 2:
                first = m * 2 * P + g * P
            else:
                first = (m // 2) * N + g * HALF + (m % 2) * P
            return slice(first, first + P)

        def w2_path(e):
            w2_tiles(e)
            if e == 0:
                gb = arena.tile([P, 2, N, 4], BF16, name="gb0_2", align_bytes=64, offset=STEP * 5)
            else:
                gb = hfirst.tile([P, 2, N, 4], BF16, name="gb1_2", align_bytes=64, offset=0)
            w2_copy("s", gb[:, 0], e, 0, 0, N)
            w2_copy("v", gb[:, 1], e, 1, 0, N)
            w2_quant(gb, e, 0, 2 * N)

        def w2_halves(e, pool, first, engines):
            w2_tiles(e)
            tiles = [pool.tile([P, 2, HALF, 4], BF16, name="half%d_%d" % (e, h), align_bytes=64, offset=first + 4096 * h) for h in range(2)]
            for g, h, engine in engines:
                w2_copy(engine, tiles[h][:, g], e, g, h * HALF, HALF)
            return tiles

        def layer1(e):
            if e == 0:
                hbs["pair"] = hfirst.tile([P, 2, 2, C, 4], BF16, name="hpair", align_bytes=64, offset=0)
            if e < 2:
                hb = hbs["pair"][:, e]
            elif e == 2:
                hb = hstage.tile([P, 2, C, 4], BF16, name="hb", align_bytes=64)
            else:
                hb = shared.tile([P, 2, C, 4], BF16, name="hb3", align_bytes=64, offset=0)
            for g2 in range(2):
                for s in range(2):
                    acc = ps1.tile([P, 4, P], F32, name="acc1")
                    for t in range(4):
                        cols = slice(t * 256 + g2 * P, t * 256 + (g2 + 1) * P)
                        nc.tensor.matmul_mx(
                            out=acc[:, t, :],
                            lhsT=w1c[e][:, cols].bitcast(FP8X4),
                            lhsT_scale=w1s[e][:, cols],
                            rhs=xc[e // 2][:, (e % 2) * C + s * P:(e % 2) * C + (s + 1) * P].bitcast(FP8X4),
                            rhs_scale=xs[e // 2][:, (e % 2) * C + s * P:(e % 2) * C + (s + 1) * P],
                            start=True,
                            stop=True,
                        )
                    nc.scalar.activation(out=hb[:, g2, s * P:(s + 1) * P, :], in_=acc[:].rearrange("p t n -> p n t"), func=GELU)
            hbs[e] = hb

        def h_quant_first():
            codes = keep.tile([P, 4 * C], U32, name="hc01", align_bytes=64)
            scales = arena.tile([P, 4 * C], U8, name="hs01", align_bytes=64, offset=STEP * 3)
            nc.vector.quantize_mx(out=codes[:].bitcast(FP8X4), scales=scales[:], in_=hbs["pair"][:].rearrange("p e g n t -> p (e g n t)"))
            for e in range(2):
                hc[e] = codes[:, e * 2 * C:(e + 1) * 2 * C]
                hs[e] = scales[:, e * 2 * C:(e + 1) * 2 * C]

        def h_quant(e):
            codes = keep.tile([P, 2 * C], U32, name="hc%d" % e, align_bytes=64)
            if e == 2:
                scales = arena.tile([P, 2 * C], U8, name="hs2", align_bytes=64, offset=STEP * 5)
            else:
                scales = shared.tile([P, 2 * C], U8, name="hs3", align_bytes=64, offset=8192)
            nc.vector.quantize_mx(out=codes[:].bitcast(FP8X4), scales=scales[:], in_=hbs[e][:].rearrange("p g n t -> p (g n t)"))
            hc[e] = codes[:]
            hs[e] = scales[:]

        def l2_pass(acc, e, g, m):
            cols = w2_columns(e, g, m)
            nc.tensor.matmul_mx(
                out=acc,
                lhsT=w2c[e][:, cols].bitcast(FP8X4),
                lhsT_scale=w2s[e][:, cols],
                rhs=hc[e][:, g * C:(g + 1) * C].bitcast(FP8X4),
                rhs_scale=hs[e][:, g * C:(g + 1) * C],
                start=(g == 0),
                stop=(g == 1),
            )

        banks = {}

        def layer2(e, m):
            if e == 0:
                banks[m] = ps2.tile([P, 2, C], F32, name="acc2")
            elif e == 2:
                late_banks[m] = ps1.tile([P, 2, C], F32, name="acc1")
            for g in range(2):
                l2_pass((banks if e < 2 else late_banks)[m][:, e % 2, :], e, g, m)

        late_banks = {}

        def evacuate(m, pair):
            if pair == 0:
                pool, offset = ((arena, STEP * 6), (arena, STEP * 6 + 4096), (hfirst, 4096), (shared, 8192))[m]
                y[m] = pool.tile([P, E * C], F32, name="y%d" % m, align_bytes=64, offset=offset)
            bank = (banks, late_banks)[pair][m]
            copy_on("s", y[m][:, pair * 2 * C:(pair + 1) * 2 * C], bank[:].rearrange("p a c -> p (a c)"))

        def evacuate_first(e):
            copy_on("s", y[0][:, e * C:(e + 1) * C], late_banks[0][:, e - 2, :])

        def combine(m):
            a = fin.tile([P, T], F32, name="prod_a")
            b = fin.tile([P, T], F32, name="prod_b")
            o = results.tile([P, T], F32, name="res")
            nc.vector.tensor_tensor(a[:], y[m][:].indirect(pos1_t[:]), gates[m][:, 0, :], MULT)
            if m >= PE_ADD:
                half = T // 2
                for i in range(2):
                    cols = slice(i * half, (i + 1) * half)
                    nc.vector.tensor_tensor(b[:, cols], y[m][:].indirect(pos2_t[:, i * (half // 16):(i + 1) * (half // 16)]), gates[m][:, 1, cols], MULT)
                    nc.vector.tensor_tensor(o[:, cols], a[:, cols], b[:, cols], ADD)
                    nc.sync.dma_start(out[m * P:(m + 1) * P, cols], o[:, cols])
                return
            nc.vector.tensor_tensor(b[:], y[m][:].indirect(pos2_t[:]), gates[m][:, 1, :], MULT)
            parts = 2 if m == PE_ADD - 1 else 1
            spans = [slice(i * T // parts, (i + 1) * T // parts) for i in range(parts)]
            totals = [ps2.tile([P, T // parts], F32, name="acc2") for cols in spans]
            for prod in (a, b):
                for total, cols in zip(totals, spans):
                    nc.tensor.matmul(out=total[:], lhsT=ident[:], rhs=prod[:, cols], start=prod is a, stop=prod is b)
            for total, cols in zip(totals, spans):
                nc.scalar.copy(out=o[:, cols], in_=total[:])
                nc.sync.dma_start(out[m * P:(m + 1) * P, cols], o[:, cols])

        x_gather()
        w1_path(0)
        x_path(0)
        load_w2(2)
        layer1(0)
        w1_path(1)
        x_path(1)
        load_w2(3)
        load_last_half(0)
        layer1(1)
        w1_path(2)
        load_first_gate(0)
        load_last_half(1)
        load_first_gate(1)
        load_gates(1, 4)
        layer1(2)
        w1_path(3)
        h_quant_first()
        layer1(3)
        for e in range(2):
            w2_path(e)
            h_quant(2 + e)
            for m in range(4):
                layer2(e, m)
        tiles = w2_halves(2, arena, STEP * 6, ((0, 0, "s"), (0, 1, "s"), (1, 0, "v"), (1, 1, "s")))
        for h in range(2):
            w2_quant(tiles[h], 2, h * N, N)
            for m in (2 * h, 2 * h + 1):
                layer2(2, m)
                if m == 0:
                    evacuate(0, 0)
                    evacuate_first(2)
        w2_tiles(3)
        for m in range(2):
            block = hfirst.tile([P, 2, P, 4], BF16, name="block%d" % m, align_bytes=64, offset=2048 * m)
            copy_on(
                "v",
                block[:].rearrange("p g (c i) j -> p g c j i", i=4),
                raw_whole[3][:, :, :, m * P:(m + 1) * P].rearrange("p g j (c i) -> p g c j i", i=4),
            )
            blocks.append(block)
        second = hfirst.tile([P, 2, HALF, 4], BF16, name="second", align_bytes=64, offset=4096)
        w2_copy("v", second[:, 0], 3, 0, HALF, HALF)
        w2_copy("s", second[:, 1], 3, 1, HALF, HALF)
        for m in range(2):
            w2_quant(blocks[m], 3, m * 2 * P, 2 * P)
            layer2(3, m)
            if m == 0:
                evacuate_first(3)
            else:
                evacuate(m, 0)
                evacuate(m, 1)
        w2_quant(second, 3, N, N)
        for m in (2, 3):
            layer2(3, m)
            evacuate(m, 0)
            evacuate(m, 1)
        for m in range(4):
            combine(m)
